import numpy as np, ml_dtypes
CORES = [113,118,241,246]
N = 4
BF = ml_dtypes.bfloat16
def gentries(a):
    return np.ascontiguousarray(a.reshape(8, 16, -1).transpose(0, 2, 1)).reshape(8, -1)
def gtable(e):
    e = np.asarray(e); return np.ascontiguousarray(e.reshape(8, -1, 16).transpose(0, 2, 1)).reshape(128, -1).astype(np.int32)
V, D, M, R = 2048, 4, 64, 2
def joined(x):
    return np.stack([gentries(x[r]).reshape(8, D, V) for r in range(N)], 2).reshape(8, D, N * V)
def pack(p, a, w):
    pin, inc = [np.stack([gtable(x.reshape(8, D, N, V)[:, :, r].reshape(8, D * V)) for r in range(N)]) for x in (p, np.argsort(p, -1))]
    return {"part": np.ascontiguousarray(a.transpose(1, 0, 2)).astype(np.int32), "pin": pin, "inc": inc, "w": np.ascontiguousarray(w).astype(np.int32)}
def mix(rng, p, share):
    p = np.array(p); s = np.flatnonzero(rng.random(p.size) < share); p[s] = rng.permutation(p[s]); return p
def clusters(rng, noise):
    p = np.zeros((8, D, N * V), np.int64); h = rng.integers(0, 16, (8, N * V))
    for g in range(8):
        e = np.argsort(rng.permutation(h[g]), kind="stable")
        for i in range(D):
            p[g, i, e] = np.lexsort((rng.random(N * V), h[g])); p[g, i] = mix(rng, p[g, i], noise[g])
    return p, h
def spoil(rng, h, share):
    return np.where(rng.random((8, N, V)) < share, rng.integers(0, 16, (8, N, V)), h.reshape(8, N, V))
def setup_inputs(rng):
    p, h = clusters(rng, rng.random(8) * 0.15)
    return pack(p, spoil(rng, h, rng.random((8, N, 1)) * 0.3), rng.integers(0, 16, (N, 8, V)))
def setup_inputs_ties(rng):
    p = np.stack([np.stack([rng.permutation(N * V) for i in range(D)]) for g in range(8)])
    w = rng.integers(1, 16, (1, 8, 1)) * np.where(np.arange(8)[None, :, None] & 1, rng.integers(0, 2, (N, 8, V)), 1)
    return pack(p, rng.integers(0, 16, (8, N, V)), w)
def setup_inputs_cap(rng):
    n = rng.random(8) * 0.15; n[:3] = 0; p, h = clusters(rng, n); a = spoil(rng, h, rng.random((8, N, 1)) * 0.3)
    w = rng.integers(0, 16, (N, 8, V)); w[:, :3] = np.maximum(w[:, :3], 1); inv = np.argsort(p, -1)
    for g in range(3):
        m = np.array(h[g]); busy = np.zeros(N * V, bool); want = np.roll(np.array([M, M + 1, M - 1, 0, M, 1, M + 1, M // 2])[:N], g)
        for r in range(N):
            left = int(want[r])
            for v in rng.permutation(V // 2) * 2 + (r * V + (g == 2)):
                if left == 0: break
                e = inv[g, :, v]
                if busy[e].any() or len(set(e.tolist())) < D: continue
                busy[e] = True; m[v] = (h[g, v] + rng.integers(1, 16)) & 15; left -= 1
        a[g] = m.reshape(N, V)
    return pack(p, a, w)
def setup_inputs_twins(rng):
    p = np.zeros((8, D, N * V), np.int64); j = np.arange(N * V); a = np.zeros((8, N, V), np.int64)
    for g in range(8):
        b = j if g == 0 else (j + V) % (N * V) if g == 1 else rng.permutation(N * V); s = 0.3 + 0.5 * rng.random()
        for i in range(D): p[g, i] = b if i == 0 else mix(rng, b, s)
        u = rng.permutation(16)[:rng.integers(2, 17)]; a[g] = u[rng.integers(0, u.size, (N, V))]
    return pack(p, a, rng.integers(0, 16, (N, 8, V)))
def setup_inputs_spread(rng):
    p, h = clusters(rng, rng.random(8)); k = 2.0 ** rng.integers(0, 5, (8, N, 1))
    q = np.minimum((16 * rng.random((8, N, V)) ** k).astype(np.int64), 15)
    a = np.where(rng.random((8, N, V)) < rng.random((8, N, 1)), q, h.reshape(8, N, V))
    w = np.where(rng.random((N, 8, V)) < rng.random((N, 8, 1)), rng.choice(np.array([0, 15]), (N, 8, V)), rng.integers(0, 16, (N, 8, V)))
    return pack(p, a, w)
def check_inputs(d):
    bad = [n for n, top in (("part", 16), ("pin", N * V), ("inc", N * V), ("w", 16)) if np.min(d[n]) < 0 or np.max(d[n]) >= top]
    if not bad:
        p, q, j = joined(d["pin"]), joined(d["inc"]), np.arange(N * V)
        if (np.sort(p, -1) != j).any(): bad.append("every vertex once at each position of pin")
        elif (np.take_along_axis(q, p, -1) != j).any(): bad.append("inc is the inverse of pin")
    return bad
def counts(a, p):
    return np.sum(a[p][None] == np.arange(16)[:, None, None], 1)
def reference(part, pin, inc, w):
    a = np.array(part.transpose(1, 0, 2)).reshape(8, N * V).astype(np.int64); wt = np.array(w.transpose(1, 0, 2)).reshape(8, N * V).astype(np.int64)
    p, e, j = joined(pin), joined(inc), np.arange(N * V); cut = np.zeros(8, np.int64)
    for g in range(8):
        for t in range(R):
            c = counts(a[g], p[g]); one = wt[g] * (c == 1); none = wt[g] * (c == 0)
            gain = np.sum(one[np.broadcast_to(a[g], (D, N * V)), e[g]], 0) - np.sum(none[:, e[g]], 1)
            gain[a[g], j] = -1000000
            best = np.argmax(gain, 0)
            can = ((gain[best, j] > 0) & (((j % V) + t) % 2 == 0)).reshape(N, V)
            go = (can & (np.add.accumulate(can.astype(np.int64), 1) <= M)).reshape(-1)
            a[g] = np.where(go, best, a[g])
        cut[g] = np.sum(wt[g] * (np.sum(counts(a[g], p[g]) > 0, 0) - 1))
    return {"newpart": np.ascontiguousarray(a.reshape(8, N, V).transpose(1, 0, 2)).astype(np.float32), "cut": np.repeat(cut.astype(np.float32)[None, :, None], N, 0)}

@@ -1,0 +1,577 @@
+from concourse.bass import DstId, RemoteDMATransfer
+from concourse.mybir import AluOpType as ALU, AxisListType, ActivationFunctionType as ACT
+
+F32, BF, I32, U16 = "float32", "bfloat16", "int32", "uint16"
+TW = 8448
+
+SCRATCH = {"DP": ("dram", [4, 128, 128], U16), "DI": ("dram", [4, 128, 128], F32)}
+for _t, _l in (
+    (I32, "P32 128,W32 128,PIN32 512,INC32 512,SC 1024,YI 4 2 8,KI 1,CI 4"),
+    (U16, "PU 512,PINU 512,OT0 256,OT1 256,OFC 16,OFQ 4,OF 64"),
+    (F32, "IF 512,IW0 256,IW1 256,IW 4 2 64,IWF 4 2 64,TC 64,CUM 64,ACC 4,EI 256,SC2 256,RL 256,FD 4,CACC 4,WS 4,"
+          "NA 64,OUTB 4 16 2,NPR 128,CUTS 4,CUTR 16,CF 32,ROW 16,ROW2 16,ONE 256,PT 512,PX 128,D0 256,SIG 64,BOW 256,"
+          "D2 256,IWR 256,HW 2"),
+    (BF, "PB 512,WB 512,WIN 8192,G 8192,S 8448,M 8448,GV 4096,L 8 2 8,FL 64,YB 80,ZB 80,COLB 4,EQ 64,E 256,EY 64,TH 256,"
+         "RO 256,DL 256,TMP 256,MG 768,NB 64,SG 64,LN 256,A 128,SEL 1024,X 128,T1 128,T2 128,T3 128,DM 128,SUMR 32,TIE 32,"
+         "CSW 224,ONEB 256,CIND 64,BO 128,UN 128,PQ 512,BQ 512,SH 128,BA 128,BB 256,MO 128,DD 128,THM 128,QL 64,IZ 224,"
+         "ZER 128,IP 128,IM 128,IS 128"),
+):
+    for _e in _l.split(","):
+        SCRATCH[_e.split()[0]] = ("sbuf", [128] + [int(_x) for _x in _e.split()[1:]], _t)
+for _b in range(8):
+    SCRATCH["ps%d" % _b] = ("psum", [128, 512], F32)
+NDMA = 44
+SEMAPHORES = (["eV", "eS", "eP", "eG", "sent"] + ["dm%d" % k for k in range(NDMA)]
+              + ["%s%d" % (m, s) for m in ("ap", "aw", "apin", "ainc", "anp", "acut") for s in range(4)])
+
+
+def rank_program(g, core, T, topo):
+    d = T.rank_of(core)
+    if d is None:
+        return
+    Q = {"V": g.vector, "S": g.scalar, "P": g.tensor, "G": g, "Y": g.sync}
+    count = {"V": 0, "S": 0, "P": 0, "G": 0}
+    seen = {q: {} for q in Q}
+    recs = {}
+    total = {}
+    ndma = [0]
+
+    def R(name, *idx):
+        shape = SCRATCH[name][1][1:]
+        part = slice(None)
+        if idx and isinstance(idx[0], tuple):
+            part = slice(idx[0][0], idx[0][1])
+            idx = idx[1:]
+        idx = list(idx) + [slice(None)] * (len(shape) - len(idx))
+        cols = [0]
+        for n, ix in zip(shape, idx):
+            r = range(n)[ix] if isinstance(ix, slice) else range(ix, ix + 1)
+            cols = [c * n + k for c in cols for k in r]
+        rows = range(128)[part]
+        gaps = set(cols) if cols[-1] - cols[0] + 1 != len(cols) else None
+        return (T[name][tuple([part] + idx)], name, (cols[0], cols[-1], rows[0], rows[-1], gaps), None)
+
+    def meet(a, b):
+        if a[1] < b[0] or b[1] < a[0] or a[3] < b[2] or b[3] < a[2]:
+            return False
+        return a[4] is None or b[4] is None or not a[4].isdisjoint(b[4])
+
+    def C(a, b, step=None):
+        return slice(a, b, step)
+
+    def W(a, n):
+        return slice(a, a + n)
+
+    def IND(win, off):
+        return (win[0].indirect(off[0]), win[1], win[2], off)
+
+    def wait(q, sem, n):
+        if seen[q].get(sem, 0) < n:
+            Q[q].wait_ge(T.sem[sem], n)
+            seen[q][sem] = n
+
+    def order(q, outs, ins, dma=False):
+        need = {}
+        ins = list(ins)
+        for x in outs + ins[:]:
+            if x[3] is not None:
+                ins.append(x[3])
+        for wr, lst in ((True, outs), (False, ins)):
+            for x in lst:
+                bank = x[1].startswith("ps")
+                for (span, w, ev, eq) in recs.get(x[1], []):
+                    same = eq == q and not dma
+                    if bank and (q == "P" or not same):
+                        hit = not same
+                    else:
+                        hit = (wr or w) and meet(span, x[2])
+                    if hit:
+                        need[ev[0]] = max(need.get(ev[0], 0), ev[1])
+        for s, n in need.items():
+            wait(q, s, n)
+        return ins
+
+    def note(q, outs, ins, ev):
+        for x in outs:
+            recs.setdefault(x[1], []).append((x[2], True, ev, q))
+        for x in ins:
+            recs.setdefault(x[1], []).append((x[2], False, ev, q))
+        total[ev[0]] = max(total.get(ev[0], 0), ev[1])
+
+    def ap(x):
+        return x[0] if isinstance(x, tuple) else x
+
+    def emit(q, make, outs, ins):
+        ins = order(q, outs, [x for x in ins if isinstance(x, tuple)])
+        if q == "G":
+            wait("G", "eG", count["G"])
+        count[q] += 1
+        make().then_inc(T.sem["e" + q], 1)
+        note(q, outs, ins, ("e" + q, count[q]))
+
+    def copy(o, i): emit("V", lambda: g.vector.tensor_copy(o[0], i[0]), [o], [i])
+    def tt(o, a, b, op): emit("V", lambda: g.vector.tensor_tensor(o[0], a[0], b[0], op), [o], [a, b])
+    def memset(o, c): emit("V", lambda: g.vector.memset(o[0], c), [o], [])
+
+    def ts(o, a, s1, op0, s2=None, op1=None):
+        if op1 is None:
+            emit("V", lambda: g.vector.tensor_scalar(o[0], a[0], ap(s1), None, op0), [o], [a, s1])
+        else:
+            emit("V", lambda: g.vector.tensor_scalar(o[0], a[0], ap(s1), ap(s2), op0, op1), [o], [a, s1, s2])
+
+    def scan(o, a, b, init, op0, op1):
+        emit("V", lambda: g.vector.tensor_tensor_scan(o[0], a[0], b[0], init, op0, op1), [o], [a, b])
+
+    def act(o, i, f, bias=None, scale=None, acc=None):
+        kw = {}
+        if bias is not None: kw["bias"] = ap(bias)
+        if scale is not None: kw["scale"] = ap(scale)
+        if acc is not None: kw["accum_out"] = acc[0]
+        emit("S", lambda: g.scalar.activation(o[0], i[0], f, **kw), [o] + ([acc] if acc else []), [i, bias, scale])
+
+    def lin(o, i, scale=None, bias=None): act(o, i, ACT.Identity, bias=bias, scale=scale)
+
+    def mm(o, l, r, start=True, stop=True):
+        emit("P", lambda: g.tensor.matmul(o[0], l[0], r[0], start, stop), [o], [l, r])
+
+    def iota(o, pat, base, cm=0):
+        if SCRATCH[o[1]][2] == I32:
+            emit("G", lambda: g.iota(o[0], pat, base, cm), [o], [])
+        else:
+            emit("G", lambda: g.iota(o[0], pat, base, cm, allow_small_or_imprecise_dtypes=True), [o], [])
+
+    def sel(o, i, pat, op, fill, base, cm=1):
+        emit("G", lambda: g.affine_select(o[0], i[0], pat, op, float(fill), base, cm), [o], [i])
+
+    def dma(q, o, i):
+        outs = [o] if isinstance(o, tuple) else []
+        ins = order(q, outs, [i] if isinstance(i, tuple) else [], True)
+        s = "dm%d" % ndma[0]
+        ndma[0] += 1
+        Q[q].dma_start(ap(o), ap(i)).then_inc(T.sem[s], 16)
+        note("D", outs, ins, (s, 16))
+
+    def load(q, name, src):
+        for a in range(2):
+            dma(q[a], R(name, (64 * a, 64 * a + 64)), src[:, 1024 * a:1024 * a + 1024])
+
+    def masks(r):
+        me = T.cores[r]
+        far = [s for s in range(4) if T.cores[s] not in topo.cores_of(me)]
+        used, out = [], {}
+        for k, s in enumerate(far):
+            e = topo.engines(me, T.cores[s])
+            n = len(e) // len(far)
+            out[s] = e[k * n:(k + 1) * n]
+            used += out[s]
+        for s in range(4):
+            if s != r and s not in far:
+                out[s] = [e for e in topo.engines(me, T.cores[s]) if e not in used][:len(used) // 2]
+        return out
+
+    mine = masks(d)
+    others = sorted(mine, key=lambda s: (T.cores[s] not in topo.cores_of(core), s))
+    sent = [0]
+
+    def send(tag, src, dst):
+        srcs = [src(s) for s in others]
+        order("G", [], srcs, True)
+        trs = []
+        for s, x in zip(others, srcs):
+            rid, pid = topo.addr(T.cores[s], core)
+            trs.append(RemoteDMATransfer(dst_ids=[DstId(rid=rid, pnc=pid)], dma_engine_mask=sum(1 << e for e in mine[s]),
+                                         remote_sem=T.sem["%s%d" % (tag, d)], src=x[0], dst=dst(d)[0]))
+            sent[0] += len(mine[s])
+        g.remote_dma_fused(trs, local_sem=T.sem.sent)
+        total["sent"] = sent[0]
+        for s in others:
+            note("D", [dst(s)], [], ("%s%d" % (tag, s), len(masks(s)[d])))
+
+    def dram(name, s):
+        return (T[name][s], name, (0, 3, 0, 127, None), None)
+
+    def stage(name, i, src):
+        dma("Y", (T[name][:, 32 * i:32 * i + 32, :], name, (i, i, 0, 127, None), None), src)
+
+    def slot(name, n=128):
+        return lambda s: R(name, W(n * s, n))
+
+    def ps(b, *idx): return R("ps%d" % b, *idx)
+    def cf(k, n=1): return R("CF", W(k, n))
+    LAM, HH, JJ, XX, RAMP, THB, CX, LH, SG4, MX, MH, CB, CM, HS4, HSM, B1, B2, JQ = (
+        0, 1, 2, 3, 4, 5, 6, 7, 8, 12, 14, 16, 17, 18, 20, 22, 24, 26)
+
+    load("YS", "P32", T.part)
+    dma("S", R("INC32"), T.inc[:])
+    load("YY", "W32", T.w)
+    dma("Y", R("PIN32"), T.pin[:])
+    iota(R("KI"), [[0, 1]], 0, 1)
+    for a in (0, 64):
+        iota(R("A", (a, a + 64)), [[0, 4], [-8, 2], [0, 16]], -16 * d, 1)
+    iota(R("X"), [[0, 4], [-100, 2], [-1, 16]], 0)
+    iota(R("ROW"), [[1, 16]], 0)
+    iota(R("PX"), [[-16, 8], [-1000, 2], [-2, 8]], 0, 1)
+    memset(R("TIE", (64, 128)), 0.0)
+    memset(R("YB", C(64, 80)), 0.0)
+    memset(R("ZB", C(64, 80)), 0.0)
+    ts(R("CI", C(0, 1)), R("KI"), 15, ALU.bitwise_and)
+    ts(R("CI", C(1, 2)), R("KI"), 4, ALU.logical_shift_right, 1, ALU.bitwise_and)
+    ts(R("CI", C(2, 3)), R("KI"), 5, ALU.logical_shift_right)
+    ts(R("CI", C(3, 4)), R("KI"), 1, ALU.bitwise_and)
+    copy(cf(0, 4), R("CI"))
+    lin(cf(CX), cf(HH), 100.0, cf(LAM))
+    lin(cf(RAMP), cf(LAM), -1.0, 1.0)
+    lin(cf(THB), cf(LAM), -16.0, 0.5)
+    lin(cf(LH), cf(LAM), None, 0.5)
+    lin(cf(CB), cf(JJ), 128.0, 64.0)
+    act(cf(CM), cf(RAMP), ACT.Relu, scale=112.0)
+    for c in range(6):
+        ts(R("SEL", W(128 * c, 128)), R("A"), float(c), ALU.is_equal)
+    lin(R("X"), R("X"), None, cf(CX))
+    lin(cf(CM), cf(CM), -1.0, -8.0)
+    lin(cf(SG4, 4), R("ROW", C(0, 4)), 16.0, cf(LH))
+    copy(slot("PB")(d), R("P32"))
+    send("ap", lambda s: slot("PB")(d), slot("PB"))
+    copy(slot("WB")(d), R("W32"))
+    send("aw", lambda s: slot("WB")(d), slot("WB"))
+    for c in range(6, 8):
+        ts(R("SEL", W(128 * c, 128)), R("A"), float(c), ALU.is_equal)
+    ts(cf(MX, 2), R("ROW", C(0, 2)), cf(XX), ALU.is_equal)
+    ts(cf(MH, 2), R("ROW", C(0, 2)), cf(HH), ALU.is_equal)
+    ts(cf(JQ, 4), R("ROW", C(0, 4)), cf(JJ), ALU.is_equal)
+    for k in range(4):
+        ts(R("PT", W(128 * k, 128)), R("PX"), float(k // 2 - 1000 * (k % 2)), ALU.is_equal)
+    for k, v in ((HS4, -0.25), (HSM, -1.0), (B1, -191.0), (B2, 2529.0)):
+        lin(cf(k, 2), cf(MH, 2), v)
+    copy(R("IF"), R("INC32"))
+    copy(R("PU"), R("PIN32"))
+    for i in range(4):
+        stage("DP", i, R("PU", W(128 * i, 128)))
+    for i in range(4):
+        dma("Y", R("PINU", (32 * i, 32 * i + 32), W(128 * d, 128)), R("PU", (32 * d, 32 * d + 32), W(128 * i, 128)))
+    ts(R("T1"), R("X"), 0.0, ALU.is_equal, -32.0, ALU.mult)
+    ts(R("T2"), R("X"), 1.0, ALU.is_equal, 64.0, ALU.mult)
+    ts(R("T3"), R("X"), 2.0, ALU.is_equal, -32.0, ALU.mult)
+    tt(R("T1"), R("T1"), R("T2"), ALU.add)
+    ts(R("SUMR"), R("X", C(0, 32)), 0.0, ALU.is_equal, 512.0, ALU.mult)
+    tt(R("DM"), R("T1"), R("T3"), ALU.add)
+    for j in range(4):
+        memset(R("DM", (32 * j, 32 * j + 32), W(32 * j, 32)), 0.0)
+
+    blk = [[-16, 8], [0, 16]]
+    nblk = [[16, 8], [0, 16]]
+    ID = R("IZ", C(96, 224))
+
+    def inblock(o, i):
+        sel(o, i, blk, ALU.is_ge, 0, 0)
+        sel(o, o, nblk, ALU.is_ge, 0, 15, -1)
+
+    iota(R("ONE"), [[0, 256]], 1)
+    iota(R("ONEB"), [[0, 256]], 1)
+    iota(R("ZER"), [[0, 128]], 0)
+
+    def constants_a():
+        sel(R("TIE", (32, 64)), R("ONEB", (32, 64), C(0, 32)), [[-16, 2], [0, 16]], ALU.is_equal, 0, -1)
+        for k, v in ((0, 496), (1, -496)):
+            sel(R("TIE", (64, 96)), R("TIE", (64, 96)), [[-16, 2], [0, 16]], ALU.not_equal, v, -k)
+        iota(R("ROW2"), [[1, 16]], 512)
+        iota(R("SH"), [[0, 4], [1, 2], [0, 16]], 0)
+        iota(R("D2"), [[0, 256]], -1000000)
+        iota(R("D0"), [[0, 256]], -16)
+
+    def constants_b():
+        sel(R("D0"), R("D0"), [[0, 16], [1, 16]], ALU.not_equal, 65536, 0, 0)
+        inblock(R("BO"), R("ONEB", C(0, 128)))
+        sel(R("IZ"), R("ONEB", C(0, 224)), [[-1, 224]], ALU.is_equal, 0, 96)
+        sel(R("CIND"), R("ONEB", C(0, 64)), [[-2, 64]], ALU.is_ge, 0, 0)
+        sel(R("CIND"), R("CIND"), [[2, 64]], ALU.is_ge, 0, 1, -1)
+        sel(R("UN"), R("ZER"), [[1, 128]], ALU.is_ge, -1, 0, -1)
+        sel(R("UN"), R("UN"), nblk, ALU.is_ge, 0, 15, -1)
+        sel(R("BA", (0, 16)), R("ONEB", (0, 16), C(0, 128)), [[0, 8], [-1, 16]], ALU.is_equal, 0, 0)
+        iota(R("BB", (0, 16)), [[0, 256]], 81920)
+        sel(R("BB", (0, 16)), R("BB", (0, 16)), [[0, 16], [-1, 16]], ALU.not_equal, 16384, 0)
+        iota(R("SIG"), [[1, 64]], 1)
+        for q in range(4):
+            sel(R("PQ", W(128 * q, 128)), R("ONEB", C(0, 128)), [[0, 4], [-1, 32]], ALU.is_equal, 0, -32 * q)
+        i = R("ZER")
+        for k, v in ((0, -16), (1, 16), (-15, -16)):
+            sel(R("THM"), i, [[-1, 128]], ALU.not_equal, v, -k)
+            i = R("THM")
+        inblock(i, i)
+        sel(R("IWR"), R("ONE"), [[0, 2], [-1, 128]], ALU.is_equal, 0, 0)
+        sel(R("QL"), R("ZER", C(0, 64)), [[-32, 4], [-1, 16]], ALU.not_equal, 1, 0)
+        sel(R("QL"), R("QL"), [[-32, 4], [-1, 16]], ALU.not_equal, 1, -16)
+        iota(R("HW"), [[0, 2]], 15)
+        for a in (0, 64):
+            sel(R("HW", (a, a + 64)), R("HW", (a, a + 64)), [[-8, 2]], ALU.is_ge, 0, -16 * d)
+            sel(R("HW", (a, a + 64)), R("HW", (a, a + 64)), [[8, 2]], ALU.is_ge, 0, 16 * d + 7, -1)
+
+    def constants_c():
+        lin(R("DD"), R("ZER"))
+        for a in (0, 128):
+            lin(R("BOW", W(a, 128)), R("BO"))
+        for j in range(4):
+            lin(R("DD", (32 * j, 32 * j + 32), W(32 * j, 32)), R("DM", (32 * j, 32 * j + 32), W(32 * ((j + 1) % 4), 32)), -1.0)
+        for q in range(4):
+            lin(R("BQ", W(128 * q, 128)), R("SH"), cf(JQ + q))
+        lin(R("MO"), R("BO"), cf(CM))
+
+    def lists_send():
+        for t in range(2):
+            for cx in range(2):
+                mm(ps(6 + t, C(0, 256)), R("PT", W(128 * (2 * t + cx), 128)), R("IF", C(cx, 512, 2)), cx == 0, cx == 1)
+            lin(R("IWF", C(0, 4), t), ps(6 + t, C(0, 256)), None, -16384.0)
+        for i in range(4):
+            stage("DI", i, R("IWF", i))
+        dma("Y", R("IW", d), dram("DI", d))
+        send("apin", lambda s: dram("DP", s), slot("PINU"))
+        constants_a()
+        send("ainc", lambda s: dram("DI", s), lambda s: R("IW", s))
+        constants_b()
+
+    def lists_out(t):
+        ts(R("OT%d" % t), R("IW", C(0, 4), t), 16384.0, ALU.add)
+
+    def lists_win(t):
+        act(R("IW%d" % t), R("IW", C(0, 4), t), ACT.Copy)
+
+    def spread(bank, name, s, b, more):
+        a = 64 * (b // 2)
+        for x in range(4):
+            mm(ps(bank, W(128 * x, 128)), R("SEL", (a, a + 64), W(128 * (4 * (b % 2) + x), 128)),
+               R(name, (a, a + 64), W(128 * s, 128)), x == 0 or not more, not more)
+
+    n = 0
+    for s in [d] + others:
+        for b in range(4):
+            bank = n % 6
+            spread(bank, "PB", s, b, False)
+            o = R("WIN", W(2048 * s + 512 * b, 512))
+            if n in (4, 6, 8, 10, 12, 14):
+                ts(o, ps(bank), cf(RAMP), ALU.add, 0.0, ALU.max)
+            else:
+                act(o, ps(bank), ACT.Relu, bias=cf(RAMP))
+            if n == 3:
+                lists_send()
+            n += 1
+
+    chunks = [4 * s + b for s in [d] + others for b in range(4)]
+    banks = [0, 1, 2, 3, 4, 5, 7, 0, 1, 2, 3, 4, 5, 7, 1, 2]
+    LAG = 4
+
+    def gath(k):
+        ch = chunks[k]
+        src = IND(R("WIN"), R("PINU", W(32 * ch, 32)))
+        o = R("G", W(512 * ch, 512))
+        spread(banks[k], "WB", ch // 4, ch % 4, True)
+        if k % 2 == 0:
+            copy(o, src)
+        else:
+            act(o, src, ACT.Copy)
+        mm(ps(banks[k]), R("DM"), o, False, True)
+
+    def evac(k):
+        o = R("S", W(512 * chunks[k], 512))
+        if k % 2 == 0:
+            copy(o, ps(banks[k]))
+        else:
+            act(o, ps(banks[k]), ACT.Copy)
+
+    def ties(t, q):
+        for l in range(8):
+            mm(ps(q, W(32 * l, 32)), R("WIN", C(2048 * q + 2 * l + t, 2048 * q + 2048, 16)), R("TIE"), l == 0, False)
+
+    for k in range(16):
+        gath(k)
+        if k >= LAG:
+            evac(k - LAG)
+        if k == 5:
+            lin(R("TIE", (0, 32)), R("DM", (0, 32), C(32, 64)), 8.0)
+        if k == 12:
+            lists_out(0)
+    ties(0, 0)
+    for k in range(16 - LAG, 16):
+        evac(k)
+
+    def spare(a, n):
+        return R("G", W(a, n))
+
+    def cutmm(b, bank, zs):
+        for z in zs:
+            mm(ps(bank), R("CSW", W(96 - 32 * z, 128)), R("S", W(2048 * z + 512 * b, 512)), z == 0, z == 3)
+
+    def cutev(b, bank):
+        act(spare(512 * b, 512), ps(bank), ACT.Relu, acc=R("CACC", W(b, 1)))
+
+    def newparts(t, step):
+        if step == 0:
+            lin(R("NB"), R("YB", C(0, 64)), 1.0 / 16, 160 - 7.5 / 16)
+            act(R("NA"), R("ZB", C(0, 64)), ACT.Abs, bias=-32.5)
+            act(R("SG"), R("NA"), ACT.Sign, bias=32.0, scale=-1.0)
+        elif step == 1:
+            mm(ps(4, W(128, 64)), ID, R("NB"), True, False)
+            mm(ps(4, W(128, 64)), R("IP"), R("SG"), False, True)
+            mm(ps(4, W(192, 64)), ID, R("YB", C(0, 64)), True, False)
+            mm(ps(4, W(192, 64)), R("IS"), R("NB"), False, False)
+            mm(ps(4, W(192, 64)), R("IM"), R("SG"), False, True)
+        elif step == 2:
+            for k in range(2):
+                for h in range(2):
+                    act(R("LN", W(128 * k + 64 * h, 64)), ps(4, W(128 + 64 * k, 64)), ACT.Relu, bias=cf((B1, B2)[k] + h),
+                        scale=cf(MH + h))
+            for k in range(2):
+                mm(ps(4, W(256, 64)), R("LN", W(128 * k, 128)), R("QL"), k == 0, k == 1)
+        else:
+            lin(R("OUTB", C(0, 4), C(0, 16), t), ps(4, W(256, 64)), None, -1.0)
+
+    VC = (28, 28, 26, 30)
+    tab = R("S", C(0, 8192))
+
+    for t in range(2):
+        ot = "OT%d" % t
+        for q in range(4):
+            vc = VC[q]
+            ts(R("GV", W(1024 * q, 16 * vc)), IND(tab, R(ot, W(64 * q, vc))), 0.0, ALU.max)
+            act(R("GV", C(1024 * q + 16 * vc, 1024 * q + 1024)), IND(tab, R(ot, C(64 * q + vc, 64 * q + 64))), ACT.Relu)
+            if q > 0:
+                scan(R("SC", W(256 * q - 256, 256)), R("D0"), ps(q - 1, C(0, 256)), 0.0, ALU.add, ALU.min)
+            if t == 1:
+                cutmm(q // 2, 6 + q // 2, [2 * (q % 2), 2 * (q % 2) + 1])
+            for l in range(8):
+                mm(ps(q, W(32 * l, 32)), R("GV", C(1024 * q + l, 1024 * q + 1024, 8)), R("SUMR"), False, l == 7)
+            if t == 0 and q < 3:
+                ties(0, q + 1)
+        if t == 0:
+            ts(R("SH"), R("SH"), cf(HH), ALU.is_equal)
+            ts(R("D2", C(0, 256, 16)), R("ROW2"), 16.0, ALU.mult, cf(LAM), ALU.add)
+        scan(R("SC", C(768, 1024)), R("D0"), ps(3, C(0, 256)), 0.0, ALU.add, ALU.min)
+        if t == 1:
+            cutev(0, 6)
+            cutev(1, 7)
+            cutmm(2, 1, [0, 1, 2, 3])
+            cutev(2, 1)
+        else:
+            lists_win(0)
+            constants_c()
+        for h in range(2):
+            ts(R("YI", C(0, 4), h), R("SC", C(16 * h + 15, 1024, 32)), 511, ALU.bitwise_and)
+        for x in range(2):
+            ts(R("L", C(0, 8), x), R("YI"), 256.0, ALU.subtract, cf(MX + x), ALU.mult)
+        mm(ps(4, C(0, 64)), R("L"), R("CIND"))
+        ts(R("FL"), ps(4, C(0, 64)), 0.0, ALU.is_ge)
+        copy(R("YB", C(0, 64)), ps(4, C(0, 64)))
+        mm(ps(5, C(0, 64)), R("BO"), R("FL"))
+        mm(ps(5, C(64, 128)), R("UN"), R("FL"))
+        mm(ps(0, C(0, 256)), R("BA", (0, 16)), R("BB", (0, 16)), True, False)
+        if t == 1:
+            cutmm(3, 6, [0, 1, 2, 3])
+        scan(R("TC"), R("ONE", C(0, 64)), ps(5, C(0, 64)), 0.0, ALU.mult, ALU.add)
+        for x in range(4):
+            act(spare(3072 + 256 * t + 64 * x, 64), R("TC"), ACT.Sign, bias=cf(SG4 + x), scale=-1.0, acc=R("ACC", W(x, 1)))
+        tt(R("CUM"), R("TC"), ps(5, C(64, 128)), ALU.add)
+        tt(R("ZB", C(0, 64)), R("CUM"), R("FL"), ALU.mult)
+        ts(R("OFQ"), R("ACC"), 64.0, ALU.add, 0.5, ALU.mult)
+        ts(R("COLB"), R("ACC"), 62.0, ALU.min, cf(CB), ALU.add)
+        tt(R("EQ"), IND(R("ZB"), R("OFQ")), R("SIG"), ALU.is_equal)
+        for q in range(4):
+            mm(ps(5, W(128 + 4 * q, 4)), R("PQ", W(128 * q, 128)), R("COLB"))
+        for q in range(4):
+            mm(ps(1, W(64 * q, 64)), R("PQ", W(128 * q, 128)), R("EQ"))
+        if t == 1:
+            newparts(1, 0)
+        else:
+            act(spare(2048, 512), R("WB"), ACT.Identity, acc=R("WS", C(0, 1)))
+        tt(R("EY"), IND(R("YB"), R("OFQ")), R("EQ"), ALU.mult)
+        act(R("E"), ps(1, C(0, 256)), ACT.Copy)
+        ts(R("OFC"), ps(5, C(128, 144)), 0.5, ALU.mult)
+        if t == 0:
+            lists_out(1)
+        for bank in (2, 3):
+            for q in range(4):
+                mm(ps(bank, W(64 * q, 64)), R("BQ", W(128 * q, 128)), R("EY"), bank == 2 or q == 0, bank == 2)
+        for a in range(2):
+            tt(R("EI", W(128 * a, 128)), IND(R("IW%d" % t), R("OFC", W(8 * a, 8))), R("E", W(128 * a, 128)), ALU.mult)
+        act(R("TH"), ps(2, C(0, 256)), ACT.Sign, bias=cf(THB))
+        mm(ps(3, C(0, 256)), R("MO"), R("TH"), False, True)
+        for a in range(2):
+            mm(ps(0, W(128 * a, 128)), R("BOW", W(32 - 32 * t, 128)), R("EI", W(128 * a, 128)), False, a == 1)
+        mm(ps(2, C(0, 256)), R("THM"), R("TH"), True, False)
+        if t == 0:
+            memset(R("S", C(8192, TW)), 0.0)
+            memset(R("CSW"), 0.0)
+        scan(R("SC2"), R("D2"), ps(0, C(0, 256)), -1000000.0, ALU.max, ALU.min)
+        act(R("RO"), ps(3, C(0, 256)), ACT.Relu, bias=cf(RAMP))
+        ends = R("SC2", C(15, 256, 16))
+        copy(R("OF", C(0, 16)), ends)
+        mm(ps(2, C(0, 256)), R("DD"), R("RO"), False, True)
+        for k in range(2 + t):
+            mm(ps(1, W(16 * k, 16)), R("IWR", W(32 * k + 32, 128)), ends)
+        if t == 1:
+            newparts(1, 1)
+        act(R("DL"), ps(2, C(0, 256)), ACT.Copy)
+        if t == 0:
+            for k in range(3):
+                off = R("OF", W(16 * k, 16))
+                copy(R("TMP", C(0, 128)), IND(R("S"), R("OF", W(16 * k, 8))))
+                act(R("TMP", C(128, 256)), IND(R("S"), R("OF", W(16 * k + 8, 8))), ACT.Copy)
+                if k == 0:
+                    copy(R("OF", C(16, 48)), ps(1, C(0, 32)))
+                if k == 1:
+                    ts(R("CSW", C(96, 128)), R("X", C(0, 32)), 0.0, ALU.is_equal)
+                if k == 2:
+                    memset(R("CUTS"), 0.0)
+                    newparts(0, 3)
+                    lin(R("M", C(0, 704)), R("WIN", C(0, 704)), 0.0)
+                    for a in range(1, 12):
+                        dma("Y", R("M", W(704 * a, 704)), R("M", C(0, 704)))
+                tt(IND(R("S"), off), R("TMP"), R("DL"), ALU.add)
+                if k == 0:
+                    for name, v in (("IP", 32.0), ("IM", -32.0), ("IS", -16.0)):
+                        lin(R(name), ID, v)
+                    newparts(0, 0)
+                    newparts(0, 1)
+                if k == 1:
+                    newparts(0, 2)
+                    lists_win(1)
+                    for q in range(4):
+                        ties(1, q)
+        else:
+            copy(IND(R("M"), R("OF", C(0, 16))), R("DL"))
+            act(R("TMP"), IND(R("S"), R("OF", C(0, 16))), ACT.Copy)
+            copy(R("OF", C(16, 64)), ps(1, C(0, 48)))
+            for bank, m in ((0, "IP"), (3, "IM")):
+                mm(ps(bank, C(0, 256)), ID, R("TMP"), True, False)
+                mm(ps(bank, C(0, 256)), R(m), R("DL"), False, False)
+            newparts(1, 2)
+            newparts(1, 3)
+            send("anp", lambda s: R("OUTB", s), slot("NPR", 32))
+            fin = ps(5, (0, 2), C(0, 1))
+            mm(fin, R("HW"), R("WS", C(0, 1)), True, False)
+            for b in range(3):
+                mm(fin, cf(HS4, 2), R("CACC", W(b, 1)), False, False)
+            copy(R("MG", C(0, 256)), IND(R("M"), R("OF", C(16, 32))))
+            act(R("MG", C(512, 768)), IND(R("M"), R("OF", C(48, 64))), ACT.Copy)
+            copy(R("MG", C(256, 384)), IND(R("M"), R("OF", C(32, 40))))
+            act(R("MG", C(384, 512)), IND(R("M"), R("OF", C(40, 48))), ACT.Copy)
+            cutev(3, 6)
+            for k in (1, 3, 2):
+                for bank in (3, 0):
+                    mm(ps(bank, C(0, 256)), R("IZ", W(96 - 32 * k, 128)), R("MG", W(256 * k - 256, 256)), False, k == 2)
+            mm(fin, cf(HS4, 2), R("CACC", W(3, 1)), False, False)
+            ts(R("RL"), ps(3, C(0, 256)), -1024.0, ALU.add, 0.0, ALU.max)
+            act(spare(2560, 256), ps(0, C(0, 256)), ACT.Relu, bias=-1024.0, acc=R("FD", C(1, 2)))
+            fd, rl = R("FD", C(0, 1)), R("RL")
+            emit("V", lambda: g.vector.tensor_reduce(fd[0], rl[0], AxisListType.X, ALU.add), [fd], [rl])
+            mm(fin, cf(HSM, 2), R("FD", C(1, 2)), False, False)
+            mm(fin, cf(MH, 2), fd, False, True)
+            copy(R("CUTS", (0, 2), C(0, 1)), fin)
+            send("acut", lambda s: R("CUTS", C(0, 1)), lambda s: R("CUTR", W(4 * s, 1)))
+            dma("Y", T.newpart[2 * d:2 * d + 2, :], R("OUTB", d))
+            dma("S", T.cut[2 * d:2 * d + 2, :], R("CUTS", (0, 2), C(0, 1)))
+            for s in others:
+                dma("Y", T.newpart[2 * s:2 * s + 2, :], slot("NPR", 32)(s))
+            for s in others:
+                dma("S", T.cut[2 * s:2 * s + 2, :], R("CUTR", (0, 2), W(4 * s, 1)))
+    for s, v in total.items():
+        if not any(seen[q].get(s, 0) >= v for q in seen):
+            wait("G", s, v)

@@ -4,11 +4,11 @@ from concourse.mybir import AluOpType as ALU, AxisListType, ActivationFunctionTy
 F32, BF, I32, U16 = "float32", "bfloat16", "int32", "uint16"
 TW = 8448
 
-SCRATCH = {"DP": ("dram", [4, 128, 128], U16), "DI": ("dram", [4, 128, 128], F32)}
+SCRATCH = {"DP": ("dram", [4, 128, 128], U16), "DI0": ("dram", [4, 128, 64], F32), "DI1": ("dram", [4, 128, 64], F32)}
 for _t, _l in (
     (I32, "P32 128,W32 128,PIN32 512,INC32 512,SC 1024,YI 4 2 8,KI 1,CI 4"),
     (U16, "PU 512,PINU 512,OT0 256,OT1 256,OFC 16,OFQ 4,OF 64"),
-    (F32, "IF 512,IW0 256,IW1 256,IW 4 2 64,IWF 4 2 64,TC 64,CUM 64,ACC 4,EI 256,SC2 256,RL 256,FD 4,CACC 4,WS 4,"
+    (F32, "IF 512,IW0 256,IW1 256,IWF 512,TC 64,CUM 64,ACC 4,EI 256,SC2 256,RL 128,FD 4,CACC 4,WS 4,"
           "NA 64,OUTB 4 16 2,NPR 128,CUTS 4,CUTR 16,CF 32,ROW 16,ROW2 16,ONE 256,PT 512,PX 128,D0 256,SIG 64,BOW 256,"
           "D2 256,IWR 256,HW 2"),
     (BF, "PB 512,WB 512,WIN 8192,G 8192,S 8448,M 8448,GV 4096,L 8 2 8,FL 64,YB 80,ZB 80,COLB 4,EQ 64,E 256,EY 64,TH 256,"
@@ -20,9 +20,9 @@ for _t, _l in (
         SCRATCH[_e.split()[0]] = ("sbuf", [128] + [int(_x) for _x in _e.split()[1:]], _t)
 for _b in range(8):
     SCRATCH["ps%d" % _b] = ("psum", [128, 512], F32)
-NDMA = 44
+NDMA = 48
 SEMAPHORES = (["eV", "eS", "eP", "eG", "sent"] + ["dm%d" % k for k in range(NDMA)]
-              + ["%s%d" % (m, s) for m in ("ap", "aw", "apin", "ainc", "anp", "acut") for s in range(4)])
+              + ["%s%d" % (m, s) for m in ("ap", "aw", "apin", "ai0", "ai1", "anp", "acut") for s in range(4)])
 
 
 def rank_program(g, core, T, topo):
@@ -56,14 +56,9 @@ def rank_program(g, core, T, topo):
             return False
         return a[4] is None or b[4] is None or not a[4].isdisjoint(b[4])
 
-    def C(a, b, step=None):
-        return slice(a, b, step)
-
-    def W(a, n):
-        return slice(a, a + n)
-
-    def IND(win, off):
-        return (win[0].indirect(off[0]), win[1], win[2], off)
+    def C(a, b, step=None): return slice(a, b, step)
+    def W(a, n): return slice(a, a + n)
+    def IND(win, off): return (win[0].indirect(off[0]), win[1], win[2], off)
 
     def wait(q, sem, n):
         if seen[q].get(sem, 0) < n:
@@ -98,8 +93,7 @@ def rank_program(g, core, T, topo):
             recs.setdefault(x[1], []).append((x[2], False, ev, q))
         total[ev[0]] = max(total.get(ev[0], 0), ev[1])
 
-    def ap(x):
-        return x[0] if isinstance(x, tuple) else x
+    def ap(x): return x[0] if isinstance(x, tuple) else x
 
     def emit(q, make, outs, ins):
         ins = order(q, outs, [x for x in ins if isinstance(x, tuple)])
@@ -187,15 +181,12 @@ def rank_program(g, core, T, topo):
         for s in others:
             note("D", [dst(s)], [], ("%s%d" % (tag, s), len(masks(s)[d])))
 
-    def dram(name, s):
-        return (T[name][s], name, (0, 3, 0, 127, None), None)
+    def dram(name, s): return (T[name][s], name, (0, 3, 0, 127, None), None)
 
     def stage(name, i, src):
         dma("Y", (T[name][:, 32 * i:32 * i + 32, :], name, (i, i, 0, 127, None), None), src)
 
-    def slot(name, n=128):
-        return lambda s: R(name, W(n * s, n))
-
+    def slot(name, n=128): return lambda s: R(name, W(n * s, n))
     def ps(b, *idx): return R("ps%d" % b, *idx)
     def cf(k, n=1): return R("CF", W(k, n))
     LAM, HH, JJ, XX, RAMP, THB, CX, LH, SG4, MX, MH, CB, CM, HS4, HSM, B1, B2, JQ = (
@@ -208,8 +199,6 @@ def rank_program(g, core, T, topo):
     iota(R("KI"), [[0, 1]], 0, 1)
     for a in (0, 64):
         iota(R("A", (a, a + 64)), [[0, 4], [-8, 2], [0, 16]], -16 * d, 1)
-    iota(R("X"), [[0, 4], [-100, 2], [-1, 16]], 0)
-    iota(R("ROW"), [[1, 16]], 0)
     iota(R("PX"), [[-16, 8], [-1000, 2], [-2, 8]], 0, 1)
     memset(R("TIE", (64, 128)), 0.0)
     memset(R("YB", C(64, 80)), 0.0)
@@ -227,28 +216,27 @@ def rank_program(g, core, T, topo):
     act(cf(CM), cf(RAMP), ACT.Relu, scale=112.0)
     for c in range(6):
         ts(R("SEL", W(128 * c, 128)), R("A"), float(c), ALU.is_equal)
-    lin(R("X"), R("X"), None, cf(CX))
     lin(cf(CM), cf(CM), -1.0, -8.0)
-    lin(cf(SG4, 4), R("ROW", C(0, 4)), 16.0, cf(LH))
     copy(slot("PB")(d), R("P32"))
     send("ap", lambda s: slot("PB")(d), slot("PB"))
     copy(slot("WB")(d), R("W32"))
     send("aw", lambda s: slot("WB")(d), slot("WB"))
     for c in range(6, 8):
         ts(R("SEL", W(128 * c, 128)), R("A"), float(c), ALU.is_equal)
-    ts(cf(MX, 2), R("ROW", C(0, 2)), cf(XX), ALU.is_equal)
-    ts(cf(MH, 2), R("ROW", C(0, 2)), cf(HH), ALU.is_equal)
-    ts(cf(JQ, 4), R("ROW", C(0, 4)), cf(JJ), ALU.is_equal)
-    for k in range(4):
-        ts(R("PT", W(128 * k, 128)), R("PX"), float(k // 2 - 1000 * (k % 2)), ALU.is_equal)
-    for k, v in ((HS4, -0.25), (HSM, -1.0), (B1, -191.0), (B2, 2529.0)):
-        lin(cf(k, 2), cf(MH, 2), v)
+    iota(R("X"), [[0, 4], [-100, 2], [-1, 16]], 0)
+    iota(R("ROW"), [[1, 16]], 0)
+    for k in range(2):
+        ts(R("PT", W(128 * k, 128)), R("PX"), float(-1000 * k), ALU.is_equal)
     copy(R("IF"), R("INC32"))
     copy(R("PU"), R("PIN32"))
     for i in range(4):
         stage("DP", i, R("PU", W(128 * i, 128)))
     for i in range(4):
         dma("Y", R("PINU", (32 * i, 32 * i + 32), W(128 * d, 128)), R("PU", (32 * d, 32 * d + 32), W(128 * i, 128)))
+    ts(R("X"), R("X"), cf(CX), ALU.add)
+    ts(cf(MX, 2), R("ROW", C(0, 2)), cf(XX), ALU.is_equal)
+    ts(cf(MH, 2), R("ROW", C(0, 2)), cf(HH), ALU.is_equal)
+    ts(cf(JQ, 4), R("ROW", C(0, 4)), cf(JJ), ALU.is_equal)
     ts(R("T1"), R("X"), 0.0, ALU.is_equal, -32.0, ALU.mult)
     ts(R("T2"), R("X"), 1.0, ALU.is_equal, 64.0, ALU.mult)
     ts(R("T3"), R("X"), 2.0, ALU.is_equal, -32.0, ALU.mult)
@@ -267,6 +255,8 @@ def rank_program(g, core, T, topo):
         sel(o, o, nblk, ALU.is_ge, 0, 15, -1)
 
     iota(R("ONE"), [[0, 256]], 1)
+    for cx in range(2):
+        sel(R("PT", W(256 + 128 * cx, 128)), R("ONE", C(0, 128)), [[-16, 8], [-1000, 2], [-2, 8]], ALU.is_equal, 0, 1000 * cx - 1)
     iota(R("ONEB"), [[0, 256]], 1)
     iota(R("ZER"), [[0, 128]], 0)
 
@@ -276,13 +266,14 @@ def rank_program(g, core, T, topo):
             sel(R("TIE", (64, 96)), R("TIE", (64, 96)), [[-16, 2], [0, 16]], ALU.not_equal, v, -k)
         iota(R("ROW2"), [[1, 16]], 512)
         iota(R("SH"), [[0, 4], [1, 2], [0, 16]], 0)
-        iota(R("D2"), [[0, 256]], -1000000)
-        iota(R("D0"), [[0, 256]], -16)
 
     def constants_b():
+        iota(R("D0"), [[0, 256]], -16)
         sel(R("D0"), R("D0"), [[0, 16], [1, 16]], ALU.not_equal, 65536, 0, 0)
         inblock(R("BO"), R("ONEB", C(0, 128)))
         sel(R("IZ"), R("ONEB", C(0, 224)), [[-1, 224]], ALU.is_equal, 0, 96)
+
+    def constants_d():
         sel(R("CIND"), R("ONEB", C(0, 64)), [[-2, 64]], ALU.is_ge, 0, 0)
         sel(R("CIND"), R("CIND"), [[2, 64]], ALU.is_ge, 0, 1, -1)
         sel(R("UN"), R("ZER"), [[1, 128]], ALU.is_ge, -1, 0, -1)
@@ -290,6 +281,7 @@ def rank_program(g, core, T, topo):
         sel(R("BA", (0, 16)), R("ONEB", (0, 16), C(0, 128)), [[0, 8], [-1, 16]], ALU.is_equal, 0, 0)
         iota(R("BB", (0, 16)), [[0, 256]], 81920)
         sel(R("BB", (0, 16)), R("BB", (0, 16)), [[0, 16], [-1, 16]], ALU.not_equal, 16384, 0)
+        iota(R("D2"), [[0, 256]], -1000000)
         iota(R("SIG"), [[1, 64]], 1)
         for q in range(4):
             sel(R("PQ", W(128 * q, 128)), R("ONEB", C(0, 128)), [[0, 4], [-1, 32]], ALU.is_equal, 0, -32 * q)
@@ -307,6 +299,7 @@ def rank_program(g, core, T, topo):
             sel(R("HW", (a, a + 64)), R("HW", (a, a + 64)), [[8, 2]], ALU.is_ge, 0, 16 * d + 7, -1)
 
     def constants_c():
+        lin(cf(SG4, 4), R("ROW", C(0, 4)), 16.0, cf(LH))
         lin(R("DD"), R("ZER"))
         for a in (0, 128):
             lin(R("BOW", W(a, 128)), R("BO"))
@@ -316,24 +309,20 @@ def rank_program(g, core, T, topo):
             lin(R("BQ", W(128 * q, 128)), R("SH"), cf(JQ + q))
         lin(R("MO"), R("BO"), cf(CM))
 
-    def lists_send():
-        for t in range(2):
-            for cx in range(2):
-                mm(ps(6 + t, C(0, 256)), R("PT", W(128 * (2 * t + cx), 128)), R("IF", C(cx, 512, 2)), cx == 0, cx == 1)
-            lin(R("IWF", C(0, 4), t), ps(6 + t, C(0, 256)), None, -16384.0)
+    def lists_make(t, bank):
+        for cx in range(2):
+            mm(ps(bank, C(0, 256)), R("PT", W(128 * (2 * t + cx), 128)), R("IF", C(cx, 512, 2)), cx == 0, cx == 1)
+
+    def lists_go(t, bank):
+        lin(R("IWF", W(256 * t, 256)), ps(bank, C(0, 256)), None, -16384.0)
+        name = "DI%d" % t
         for i in range(4):
-            stage("DI", i, R("IWF", i))
-        dma("Y", R("IW", d), dram("DI", d))
-        send("apin", lambda s: dram("DP", s), slot("PINU"))
-        constants_a()
-        send("ainc", lambda s: dram("DI", s), lambda s: R("IW", s))
-        constants_b()
+            stage(name, i, R("IWF", W(256 * t + 64 * i, 64)))
+        dma("Y", slot("IW%d" % t, 64)(d), dram(name, d))
+        send("ai%d" % t, lambda s: dram(name, s), slot("IW%d" % t, 64))
 
     def lists_out(t):
-        ts(R("OT%d" % t), R("IW", C(0, 4), t), 16384.0, ALU.add)
-
-    def lists_win(t):
-        act(R("IW%d" % t), R("IW", C(0, 4), t), ACT.Copy)
+        ts(R("OT%d" % t), R("IW%d" % t), 16384.0, ALU.add)
 
     def spread(bank, name, s, b, more):
         a = 64 * (b // 2)
@@ -344,7 +333,7 @@ def rank_program(g, core, T, topo):
     n = 0
     for s in [d] + others:
         for b in range(4):
-            bank = n % 6
+            bank = n % 7
             spread(bank, "PB", s, b, False)
             o = R("WIN", W(2048 * s + 512 * b, 512))
             if n in (4, 6, 8, 10, 12, 14):
@@ -352,23 +341,28 @@ def rank_program(g, core, T, topo):
             else:
                 act(o, ps(bank), ACT.Relu, bias=cf(RAMP))
             if n == 3:
-                lists_send()
+                send("apin", lambda s: dram("DP", s), slot("PINU"))
+                constants_a()
+                lists_make(0, 7)
+                lists_go(0, 7)
+                constants_b()
             n += 1
 
     chunks = [4 * s + b for s in [d] + others for b in range(4)]
+    chunks = [chunks[k] for k in (0, 1, 2, 4, 3, 5, 6, 8, 7, 9, 10, 12, 11, 13, 14, 15)]
     banks = [0, 1, 2, 3, 4, 5, 7, 0, 1, 2, 3, 4, 5, 7, 1, 2]
     LAG = 4
 
     def gath(k):
         ch = chunks[k]
-        src = IND(R("WIN"), R("PINU", W(32 * ch, 32)))
-        o = R("G", W(512 * ch, 512))
+        n = 1 if k < 2 or k >= 14 else 2 if k % 4 >= 2 else 0
+        src = IND(R("WIN"), R("PINU", W(32 * ch, 32 * max(n, 1))))
         spread(banks[k], "WB", ch // 4, ch % 4, True)
-        if k % 2 == 0:
-            copy(o, src)
-        else:
-            act(o, src, ACT.Copy)
-        mm(ps(banks[k]), R("DM"), o, False, True)
+        if n and k % 2 == 0:
+            copy(R("G", W(512 * ch, 512 * n)), src)
+        elif n:
+            act(R("G", W(512 * ch, 512 * n)), src, ACT.Copy)
+        mm(ps(banks[k]), R("DM"), R("G", W(512 * ch, 512)), False, True)
 
     def evac(k):
         o = R("S", W(512 * chunks[k], 512))
@@ -377,11 +371,18 @@ def rank_program(g, core, T, topo):
         else:
             act(o, ps(banks[k]), ACT.Copy)
 
+    def keys(q, l): return ps(5 if q == 3 and l >= 4 else q, W(32 * l, 32))
+
     def ties(t, q):
         for l in range(8):
-            mm(ps(q, W(32 * l, 32)), R("WIN", C(2048 * q + 2 * l + t, 2048 * q + 2048, 16)), R("TIE"), l == 0, False)
+            mm(keys(q, l), R("WIN", C(2048 * q + 2 * l + t, 2048 * q + 2048, 16)), R("TIE"), l == 0 or (q, l) == (3, 4), False)
 
     for k in range(16):
+        if k == 0:
+            lists_make(1, 6)
+        if k == 2:
+            lists_go(1, 6)
+            constants_d()
         gath(k)
         if k >= LAG:
             evac(k - LAG)
@@ -393,8 +394,7 @@ def rank_program(g, core, T, topo):
     for k in range(16 - LAG, 16):
         evac(k)
 
-    def spare(a, n):
-        return R("G", W(a, n))
+    def spare(a, n): return R("G", W(a, n))
 
     def cutmm(b, bank, zs):
         for z in zs:
@@ -419,6 +419,7 @@ def rank_program(g, core, T, topo):
                 for h in range(2):
                     act(R("LN", W(128 * k + 64 * h, 64)), ps(4, W(128 + 64 * k, 64)), ACT.Relu, bias=cf((B1, B2)[k] + h),
                         scale=cf(MH + h))
+        elif step == 3:
             for k in range(2):
                 mm(ps(4, W(256, 64)), R("LN", W(128 * k, 128)), R("QL"), k == 0, k == 1)
         else:
@@ -438,26 +439,28 @@ def rank_program(g, core, T, topo):
             if t == 1:
                 cutmm(q // 2, 6 + q // 2, [2 * (q % 2), 2 * (q % 2) + 1])
             for l in range(8):
-                mm(ps(q, W(32 * l, 32)), R("GV", C(1024 * q + l, 1024 * q + 1024, 8)), R("SUMR"), False, l == 7)
+                mm(keys(q, l), R("GV", C(1024 * q + l, 1024 * q + 1024, 8)), R("SUMR"), False, l == 7 or (q, l) == (3, 3))
             if t == 0 and q < 3:
                 ties(0, q + 1)
         if t == 0:
             ts(R("SH"), R("SH"), cf(HH), ALU.is_equal)
             ts(R("D2", C(0, 256, 16)), R("ROW2"), 16.0, ALU.mult, cf(LAM), ALU.add)
-        scan(R("SC", C(768, 1024)), R("D0"), ps(3, C(0, 256)), 0.0, ALU.add, ALU.min)
+        for a in range(2):
+            scan(R("SC", W(768 + 128 * a, 128)), R("D0", C(0, 128)), ps(3 + 2 * a, W(128 * a, 128)), 0.0, ALU.add, ALU.min)
         if t == 1:
             cutev(0, 6)
             cutev(1, 7)
             cutmm(2, 1, [0, 1, 2, 3])
             cutev(2, 1)
         else:
-            lists_win(0)
             constants_c()
         for h in range(2):
             ts(R("YI", C(0, 4), h), R("SC", C(16 * h + 15, 1024, 32)), 511, ALU.bitwise_and)
         for x in range(2):
             ts(R("L", C(0, 8), x), R("YI"), 256.0, ALU.subtract, cf(MX + x), ALU.mult)
         mm(ps(4, C(0, 64)), R("L"), R("CIND"))
+        if t == 0:
+            memset(R("CSW"), 0.0)
         ts(R("FL"), ps(4, C(0, 64)), 0.0, ALU.is_ge)
         copy(R("YB", C(0, 64)), ps(4, C(0, 64)))
         mm(ps(5, C(0, 64)), R("BO"), R("FL"))
@@ -476,19 +479,20 @@ def rank_program(g, core, T, topo):
         for q in range(4):
             mm(ps(5, W(128 + 4 * q, 4)), R("PQ", W(128 * q, 128)), R("COLB"))
         for q in range(4):
-            mm(ps(1, W(64 * q, 64)), R("PQ", W(128 * q, 128)), R("EQ"))
+            mm(ps((7, 1)[q // 2], W(64 * q, 64)), R("PQ", W(128 * q, 128)), R("EQ"))
         if t == 1:
             newparts(1, 0)
         else:
             act(spare(2048, 512), R("WB"), ACT.Identity, acc=R("WS", C(0, 1)))
         tt(R("EY"), IND(R("YB"), R("OFQ")), R("EQ"), ALU.mult)
-        act(R("E"), ps(1, C(0, 256)), ACT.Copy)
+        act(R("E", C(128, 256)), ps(1, C(128, 256)), ACT.Copy)
         ts(R("OFC"), ps(5, C(128, 144)), 0.5, ALU.mult)
-        if t == 0:
-            lists_out(1)
+        copy(R("E", C(0, 128)), ps(7, C(0, 128)))
         for bank in (2, 3):
             for q in range(4):
                 mm(ps(bank, W(64 * q, 64)), R("BQ", W(128 * q, 128)), R("EY"), bank == 2 or q == 0, bank == 2)
+        if t == 1:
+            newparts(1, 1)
         for a in range(2):
             tt(R("EI", W(128 * a, 128)), IND(R("IW%d" % t), R("OFC", W(8 * a, 8))), R("E", W(128 * a, 128)), ALU.mult)
         act(R("TH"), ps(2, C(0, 256)), ACT.Sign, bias=cf(THB))
@@ -498,16 +502,16 @@ def rank_program(g, core, T, topo):
         mm(ps(2, C(0, 256)), R("THM"), R("TH"), True, False)
         if t == 0:
             memset(R("S", C(8192, TW)), 0.0)
-            memset(R("CSW"), 0.0)
+            lists_out(1)
         scan(R("SC2"), R("D2"), ps(0, C(0, 256)), -1000000.0, ALU.max, ALU.min)
         act(R("RO"), ps(3, C(0, 256)), ACT.Relu, bias=cf(RAMP))
+        if t == 1:
+            newparts(1, 2)
         ends = R("SC2", C(15, 256, 16))
         copy(R("OF", C(0, 16)), ends)
         mm(ps(2, C(0, 256)), R("DD"), R("RO"), False, True)
         for k in range(2 + t):
             mm(ps(1, W(16 * k, 16)), R("IWR", W(32 * k + 32, 128)), ends)
-        if t == 1:
-            newparts(1, 1)
         act(R("DL"), ps(2, C(0, 256)), ACT.Copy)
         if t == 0:
             for k in range(3):
@@ -520,7 +524,7 @@ def rank_program(g, core, T, topo):
                     ts(R("CSW", C(96, 128)), R("X", C(0, 32)), 0.0, ALU.is_equal)
                 if k == 2:
                     memset(R("CUTS"), 0.0)
-                    newparts(0, 3)
+                    newparts(0, 4)
                     lin(R("M", C(0, 704)), R("WIN", C(0, 704)), 0.0)
                     for a in range(1, 12):
                         dma("Y", R("M", W(704 * a, 704)), R("M", C(0, 704)))
@@ -531,39 +535,43 @@ def rank_program(g, core, T, topo):
                     newparts(0, 0)
                     newparts(0, 1)
                 if k == 1:
+                    for a, v in ((B1, -191.0), (B2, 2529.0), (HS4, -0.25), (HSM, -1.0)):
+                        lin(cf(a, 2), cf(MH, 2), v)
                     newparts(0, 2)
-                    lists_win(1)
+                    newparts(0, 3)
                     for q in range(4):
                         ties(1, q)
         else:
             copy(IND(R("M"), R("OF", C(0, 16))), R("DL"))
-            act(R("TMP"), IND(R("S"), R("OF", C(0, 16))), ACT.Copy)
-            copy(R("OF", C(16, 64)), ps(1, C(0, 48)))
-            for bank, m in ((0, "IP"), (3, "IM")):
-                mm(ps(bank, C(0, 256)), ID, R("TMP"), True, False)
-                mm(ps(bank, C(0, 256)), R(m), R("DL"), False, False)
-            newparts(1, 2)
             newparts(1, 3)
+            newparts(1, 4)
             send("anp", lambda s: R("OUTB", s), slot("NPR", 32))
+            act(R("TMP"), IND(R("S"), R("OF", C(0, 16))), ACT.Copy)
+            cutev(3, 6)
+            copy(R("OF", C(16, 64)), ps(1, C(0, 48)))
+            sums = ((3, "IM", 0, 128), (0, "IP", 0, 256), (7, "IM", 128, 128))
+            for bank, m, a, n in sums:
+                mm(ps(bank, W(a, n)), ID, R("TMP", W(a, n)), True, False)
+                mm(ps(bank, W(a, n)), R(m), R("DL", W(a, n)), False, False)
             fin = ps(5, (0, 2), C(0, 1))
             mm(fin, R("HW"), R("WS", C(0, 1)), True, False)
-            for b in range(3):
+            for b in range(4):
                 mm(fin, cf(HS4, 2), R("CACC", W(b, 1)), False, False)
             copy(R("MG", C(0, 256)), IND(R("M"), R("OF", C(16, 32))))
             act(R("MG", C(512, 768)), IND(R("M"), R("OF", C(48, 64))), ACT.Copy)
             copy(R("MG", C(256, 384)), IND(R("M"), R("OF", C(32, 40))))
             act(R("MG", C(384, 512)), IND(R("M"), R("OF", C(40, 48))), ACT.Copy)
-            cutev(3, 6)
             for k in (1, 3, 2):
-                for bank in (3, 0):
-                    mm(ps(bank, C(0, 256)), R("IZ", W(96 - 32 * k, 128)), R("MG", W(256 * k - 256, 256)), False, k == 2)
-            mm(fin, cf(HS4, 2), R("CACC", W(3, 1)), False, False)
-            ts(R("RL"), ps(3, C(0, 256)), -1024.0, ALU.add, 0.0, ALU.max)
+                for bank, m, a, n in sums:
+                    mm(ps(bank, W(a, n)), R("IZ", W(96 - 32 * k, 128)), R("MG", W(256 * k - 256 + a, n)), False, k == 2)
+            ts(R("RL"), ps(3, C(0, 128)), -1024.0, ALU.add, 0.0, ALU.max)
             act(spare(2560, 256), ps(0, C(0, 256)), ACT.Relu, bias=-1024.0, acc=R("FD", C(1, 2)))
+            act(spare(2816, 128), ps(7, C(128, 256)), ACT.Relu, bias=-1024.0, acc=R("FD", C(2, 3)))
             fd, rl = R("FD", C(0, 1)), R("RL")
             emit("V", lambda: g.vector.tensor_reduce(fd[0], rl[0], AxisListType.X, ALU.add), [fd], [rl])
             mm(fin, cf(HSM, 2), R("FD", C(1, 2)), False, False)
-            mm(fin, cf(MH, 2), fd, False, True)
+            mm(fin, cf(MH, 2), fd, False, False)
+            mm(fin, cf(MH, 2), R("FD", C(2, 3)), False, True)
             copy(R("CUTS", (0, 2), C(0, 1)), fin)
             send("acut", lambda s: R("CUTS", C(0, 1)), lambda s: R("CUTR", W(4 * s, 1)))
             dma("Y", T.newpart[2 * d:2 * d + 2, :], R("OUTB", d))
@@ -571,7 +579,7 @@ def rank_program(g, core, T, topo):
             for s in others:
                 dma("Y", T.newpart[2 * s:2 * s + 2, :], slot("NPR", 32)(s))
             for s in others:
-                dma("S", T.cut[2 * s:2 * s + 2, :], R("CUTR", (0, 2), W(4 * s, 1)))
+                dma("Y" if s == others[1] else "S", T.cut[2 * s:2 * s + 2, :], R("CUTR", (0, 2), W(4 * s, 1)))
     for s, v in total.items():
         if not any(seen[q].get(s, 0) >= v for q in seen):
             wait("G", s, v)

@@ -3,25 +3,24 @@ from concourse.mybir import AluOpType as ALU, AxisListType, ActivationFunctionTy
 
 F32, BF, I32, U16 = "float32", "bfloat16", "int32", "uint16"
 TW = 8448
+TOP = 16384.0
 
-SCRATCH = {"DP": ("dram", [4, 128, 128], U16), "DI0": ("dram", [4, 128, 64], F32), "DI1": ("dram", [4, 128, 64], F32)}
+SCRATCH = {"DI0": ("dram", [4, 128, 64], U16), "DI1": ("dram", [4, 128, 64], U16)}
 for _t, _l in (
     (I32, "P32 128,W32 128,PIN32 512,INC32 512,SC 1024,YI 4 2 8,KI 1,CI 4"),
-    (U16, "PU 512,PINU 512,OT0 256,OT1 256,OFC 16,OFQ 4,OF 64"),
-    (F32, "IF 512,IW0 256,IW1 256,IWF 512,TC 64,CUM 64,ACC 4,EI 256,SC2 256,RL 128,FD 4,CACC 4,WS 4,"
-          "NA 64,OUTB 4 16 2,NPR 128,CUTS 4,CUTR 16,CF 32,ROW 16,ROW2 16,ONE 256,PT 512,PX 128,D0 256,SIG 64,BOW 256,"
-          "D2 256,IWR 256,HW 2"),
-    (BF, "PB 512,WB 512,WIN 8192,G 8192,S 8448,M 8448,GV 4096,L 8 2 8,FL 64,YB 80,ZB 80,COLB 4,EQ 64,E 256,EY 64,TH 256,"
-         "RO 256,DL 256,TMP 256,MG 768,NB 64,SG 64,LN 256,A 128,SEL 1024,X 128,T1 128,T2 128,T3 128,DM 128,SUMR 32,TIE 32,"
-         "CSW 224,ONEB 256,CIND 64,BO 128,UN 128,PQ 512,BQ 512,SH 128,BA 128,BB 256,MO 128,DD 128,THM 128,QL 64,IZ 224,"
-         "ZER 128,IP 128,IM 128,IS 128"),
+    (U16, "PU 512,PINU 512,OS 512,OT0 256,OT1 256,OFC 16,OFQ 4,OF 64"),
+    (F32, "IF 512,IW 256,E 256,SC3 256,EI 256,SC2 256,RL 128,FD 4,CACC 4,WS 4,OUTB 4 16 2,NPR 128,CUTS 4,CUTR 16,CF 40,ROW 16,"
+          "PT 512,D0 256,SIG 64,BOW 256,D2 256,IWR 256,HW 2,RC 256"),
+    (BF, "PB 512,WB 512,WIN 8192,G 8192,S 8448,M 8448,GV 4096,LF 8 2 8,LY 8 2 8,FP 128,YB 64,ZNO 240,COLB 4,EQ 64,"
+         "EN 64,EO 64,RR 128,DL 256,TMP 256,MG 768,SG 64,LN 2 2 64,A 128,SEL 1024,X 32,T1 32,T2 32,T3 32,DM 128,"
+         "DMF 32,DLH 256,SUMR 32,TIE 32,CSW 224,ONEB 224,CC 128,BO 128,BON 128,UN 128,PQ 512,BQ 608,SH 32,BA 128,BB 128,"
+         "MC 256,QL 64,IZ 224,ZER 128,IP 128,IM 128,IS 128"),
 ):
     for _e in _l.split(","):
         SCRATCH[_e.split()[0]] = ("sbuf", [128] + [int(_x) for _x in _e.split()[1:]], _t)
-for _b in range(8):
-    SCRATCH["ps%d" % _b] = ("psum", [128, 512], F32)
-NDMA = 48
-SEMAPHORES = (["eV", "eS", "eP", "eG", "sent"] + ["dm%d" % k for k in range(NDMA)]
+for _b in range(4):
+    SCRATCH["pp%d" % _b] = ("psum", [128, 1024], F32)
+SEMAPHORES = (["eV", "eS", "eP", "sent"] + ["g%d" % k for k in range(1, 61)] + ["dm%d" % k for k in range(32)]
               + ["%s%d" % (m, s) for m in ("ap", "aw", "apin", "ai0", "ai1", "anp", "acut") for s in range(4)])
 
 
@@ -35,6 +34,7 @@ def rank_program(g, core, T, topo):
     recs = {}
     total = {}
     ndma = [0]
+    first = [0]
 
     def R(name, *idx):
         shape = SCRATCH[name][1][1:]
@@ -98,10 +98,13 @@ def rank_program(g, core, T, topo):
     def emit(q, make, outs, ins):
         ins = order(q, outs, [x for x in ins if isinstance(x, tuple)])
         if q == "G":
-            wait("G", "eG", count["G"])
+            if outs[0][2][2] != first[0]:
+                wait("G", "g%d" % count["G"], 1)
+            first[0] = outs[0][2][2]
         count[q] += 1
-        make().then_inc(T.sem["e" + q], 1)
-        note(q, outs, ins, ("e" + q, count[q]))
+        ev = ("g%d" % count[q], 1) if q == "G" else ("e" + q, count[q])
+        make().then_inc(T.sem[ev[0]], 1)
+        note(q, outs, ins, ev)
 
     def copy(o, i): emit("V", lambda: g.vector.tensor_copy(o[0], i[0]), [o], [i])
     def tt(o, a, b, op): emit("V", lambda: g.vector.tensor_tensor(o[0], a[0], b[0], op), [o], [a, b])
@@ -129,25 +132,32 @@ def rank_program(g, core, T, topo):
         emit("P", lambda: g.tensor.matmul(o[0], l[0], r[0], start, stop), [o], [l, r])
 
     def iota(o, pat, base, cm=0):
-        if SCRATCH[o[1]][2] == I32:
-            emit("G", lambda: g.iota(o[0], pat, base, cm), [o], [])
-        else:
-            emit("G", lambda: g.iota(o[0], pat, base, cm, allow_small_or_imprecise_dtypes=True), [o], [])
+        kw = {} if SCRATCH[o[1]][2] == I32 else {"allow_small_or_imprecise_dtypes": True}
+        emit("G", lambda: g.iota(o[0], pat, base, cm, **kw), [o], [])
 
     def sel(o, i, pat, op, fill, base, cm=1):
         emit("G", lambda: g.affine_select(o[0], i[0], pat, op, float(fill), base, cm), [o], [i])
 
-    def dma(q, o, i):
-        outs = [o] if isinstance(o, tuple) else []
-        ins = order(q, outs, [i] if isinstance(i, tuple) else [], True)
+    def dmas(lst):
         s = "dm%d" % ndma[0]
         ndma[0] += 1
-        Q[q].dma_start(ap(o), ap(i)).then_inc(T.sem[s], 16)
-        note("D", outs, ins, (s, 16))
+        done = []
+        for q, o, i in lst:
+            outs = [o] if isinstance(o, tuple) else []
+            ins = order(q, outs, [i] if isinstance(i, tuple) else [], True)
+            Q[q].dma_start(ap(o), ap(i)).then_inc(T.sem[s], 16)
+            done.append((outs, ins))
+        for outs, ins in done:
+            note("D", outs, ins, (s, 16 * len(lst)))
+
+    def dma(q, o, i): dmas([(q, o, i)])
 
     def load(q, name, src):
-        for a in range(2):
-            dma(q[a], R(name, (64 * a, 64 * a + 64)), src[:, 1024 * a:1024 * a + 1024])
+        dmas([(q[a], R(name, (64 * a, 64 * a + 64)), src[:, 1024 * a:1024 * a + 1024]) for a in range(2)])
+
+    def load_lists(q, name, src, s):
+        dmas([(q[i % len(q)], R(name, (32 * i, 32 * i + 32), W(128 * s, 128)), src[32 * s:32 * s + 32, 128 * i:128 * i + 128])
+              for i in range(4)])
 
     def masks(r):
         me = T.cores[r]
@@ -181,148 +191,160 @@ def rank_program(g, core, T, topo):
         for s in others:
             note("D", [dst(s)], [], ("%s%d" % (tag, s), len(masks(s)[d])))
 
-    def dram(name, s): return (T[name][s], name, (0, 3, 0, 127, None), None)
-
-    def stage(name, i, src):
-        dma("Y", (T[name][:, 32 * i:32 * i + 32, :], name, (i, i, 0, 127, None), None), src)
-
     def slot(name, n=128): return lambda s: R(name, W(n * s, n))
-    def ps(b, *idx): return R("ps%d" % b, *idx)
+
+    def ps(b, *idx):
+        p = idx[0] if idx and isinstance(idx[0], tuple) else (0, 128)
+        c = idx[-1] if idx and isinstance(idx[-1], slice) else C(0, 512)
+        a = 512 * (b % 2)
+        more = (None, "ps%d" % (b + 1), (0, c.stop - 513, p[0], p[1] - 1, None), None) if c.stop > 512 else None
+        return (T["pp%d" % (b // 2)][p[0]:p[1], a + c.start:a + c.stop], "ps%d" % b,
+                (c.start, min(c.stop, 512) - 1, p[0], p[1] - 1, None), more)
+
     def cf(k, n=1): return R("CF", W(k, n))
-    LAM, HH, JJ, XX, RAMP, THB, CX, LH, SG4, MX, MH, CB, CM, HS4, HSM, B1, B2, JQ = (
-        0, 1, 2, 3, 4, 5, 6, 7, 8, 12, 14, 16, 17, 18, 20, 22, 24, 26)
+    LAM, HH, JJ, XX, RAMP, CX, K64, AH, RB, CB, MX, MH, JQ, HS4, HSM, B1, E01, ED, DS, KF, DB, NJ = (
+        0, 1, 2, 3, 4, 5, 6, 7, 8, 9, 10, 12, 14, 18, 20, 22, 24, 26, 27, 29, 30, 32)
+    ID = R("IZ", C(96, 224))
+    def bq(q, blk): return R("BQ", W(128 * q + 96 - 32 * blk, 128))
+    def zno(k, n=80): return R("ZNO", W(80 * k, n))
 
     load("YS", "P32", T.part)
+    load("YS", "W32", T.w)
     dma("S", R("INC32"), T.inc[:])
-    load("YY", "W32", T.w)
-    dma("Y", R("PIN32"), T.pin[:])
+    for s in others:
+        load_lists("YYYS", "PIN32", T.pin, s)
+    load_lists("Y", "PIN32", T.pin, d)
     iota(R("KI"), [[0, 1]], 0, 1)
-    for a in (0, 64):
-        iota(R("A", (a, a + 64)), [[0, 4], [-8, 2], [0, 16]], -16 * d, 1)
-    iota(R("PX"), [[-16, 8], [-1000, 2], [-2, 8]], 0, 1)
-    memset(R("TIE", (64, 128)), 0.0)
-    memset(R("YB", C(64, 80)), 0.0)
-    memset(R("ZB", C(64, 80)), 0.0)
+    iota(R("A"), [[0, 4], [-8, 2], [0, 16]], -16 * d, 1)
+    iota(R("X"), [[-100, 2], [-1, 16]], 0)
+    ts(cf(K64), R("KI"), 64.0, ALU.is_ge, 64.0, ALU.mult)
     ts(R("CI", C(0, 1)), R("KI"), 15, ALU.bitwise_and)
     ts(R("CI", C(1, 2)), R("KI"), 4, ALU.logical_shift_right, 1, ALU.bitwise_and)
     ts(R("CI", C(2, 3)), R("KI"), 5, ALU.logical_shift_right)
     ts(R("CI", C(3, 4)), R("KI"), 1, ALU.bitwise_and)
+    copy(cf(KF), R("KI"))
     copy(cf(0, 4), R("CI"))
-    lin(cf(CX), cf(HH), 100.0, cf(LAM))
     lin(cf(RAMP), cf(LAM), -1.0, 1.0)
-    lin(cf(THB), cf(LAM), -16.0, 0.5)
-    lin(cf(LH), cf(LAM), None, 0.5)
-    lin(cf(CB), cf(JJ), 128.0, 64.0)
-    act(cf(CM), cf(RAMP), ACT.Relu, scale=112.0)
-    for c in range(6):
-        ts(R("SEL", W(128 * c, 128)), R("A"), float(c), ALU.is_equal)
-    lin(cf(CM), cf(CM), -1.0, -8.0)
+    lin(cf(CX), cf(HH), 100.0, cf(LAM))
+    lin(R("ROW"), R("X", C(0, 16)), -1.0)
+    lin(R("X"), R("X"), None, cf(CX))
+    lin(cf(AH), cf(HH), -8.0, cf(KF))
+    for c in range(8):
+        ts(R("SEL", W(128 * c, 128)), R("A"), cf(K64), ALU.subtract, float(c), ALU.is_equal)
     copy(slot("PB")(d), R("P32"))
     send("ap", lambda s: slot("PB")(d), slot("PB"))
-    copy(slot("WB")(d), R("W32"))
-    send("aw", lambda s: slot("WB")(d), slot("WB"))
-    for c in range(6, 8):
-        ts(R("SEL", W(128 * c, 128)), R("A"), float(c), ALU.is_equal)
-    iota(R("X"), [[0, 4], [-100, 2], [-1, 16]], 0)
-    iota(R("ROW"), [[1, 16]], 0)
-    for k in range(2):
-        ts(R("PT", W(128 * k, 128)), R("PX"), float(-1000 * k), ALU.is_equal)
-    copy(R("IF"), R("INC32"))
-    copy(R("PU"), R("PIN32"))
-    for i in range(4):
-        stage("DP", i, R("PU", W(128 * i, 128)))
-    for i in range(4):
-        dma("Y", R("PINU", (32 * i, 32 * i + 32), W(128 * d, 128)), R("PU", (32 * d, 32 * d + 32), W(128 * i, 128)))
-    ts(R("X"), R("X"), cf(CX), ALU.add)
-    ts(cf(MX, 2), R("ROW", C(0, 2)), cf(XX), ALU.is_equal)
-    ts(cf(MH, 2), R("ROW", C(0, 2)), cf(HH), ALU.is_equal)
-    ts(cf(JQ, 4), R("ROW", C(0, 4)), cf(JJ), ALU.is_equal)
+
+    def perms(t):
+        for cx in range(2):
+            sel(R("PT", W(128 * (2 * t + cx), 128)), R("IWR", C(0, 128)), [[-16, 8], [-1000, 2], [-2, 8]], ALU.is_equal, 0,
+                1000 * cx - t)
+
     ts(R("T1"), R("X"), 0.0, ALU.is_equal, -32.0, ALU.mult)
     ts(R("T2"), R("X"), 1.0, ALU.is_equal, 64.0, ALU.mult)
     ts(R("T3"), R("X"), 2.0, ALU.is_equal, -32.0, ALU.mult)
+    ts(cf(NJ, 4), R("ROW", C(0, 4)), cf(JJ), ALU.not_equal)
     tt(R("T1"), R("T1"), R("T2"), ALU.add)
+    ts(cf(E01, 2), R("ROW", C(0, 2)), cf(LAM), ALU.is_equal)
+    ts(R("SH"), R("A", C(0, 32)), float(16 * d), ALU.add, cf(AH), ALU.is_equal)
+    tt(R("DMF"), R("T1"), R("T3"), ALU.add)
     ts(R("SUMR"), R("X", C(0, 32)), 0.0, ALU.is_equal, 512.0, ALU.mult)
-    tt(R("DM"), R("T1"), R("T3"), ALU.add)
+    tt(cf(ED), cf(E01), cf(E01 + 1), ALU.subtract)
     for j in range(4):
-        memset(R("DM", (32 * j, 32 * j + 32), W(32 * j, 32)), 0.0)
-
-    blk = [[-16, 8], [0, 16]]
-    nblk = [[16, 8], [0, 16]]
-    ID = R("IZ", C(96, 224))
-
-    def inblock(o, i):
-        sel(o, i, blk, ALU.is_ge, 0, 0)
-        sel(o, o, nblk, ALU.is_ge, 0, 15, -1)
-
-    iota(R("ONE"), [[0, 256]], 1)
-    for cx in range(2):
-        sel(R("PT", W(256 + 128 * cx, 128)), R("ONE", C(0, 128)), [[-16, 8], [-1000, 2], [-2, 8]], ALU.is_equal, 0, 1000 * cx - 1)
-    iota(R("ONEB"), [[0, 256]], 1)
-    iota(R("ZER"), [[0, 128]], 0)
-
-    def constants_a():
-        sel(R("TIE", (32, 64)), R("ONEB", (32, 64), C(0, 32)), [[-16, 2], [0, 16]], ALU.is_equal, 0, -1)
-        for k, v in ((0, 496), (1, -496)):
-            sel(R("TIE", (64, 96)), R("TIE", (64, 96)), [[-16, 2], [0, 16]], ALU.not_equal, v, -k)
-        iota(R("ROW2"), [[1, 16]], 512)
-        iota(R("SH"), [[0, 4], [1, 2], [0, 16]], 0)
-
-    def constants_b():
-        iota(R("D0"), [[0, 256]], -16)
-        sel(R("D0"), R("D0"), [[0, 16], [1, 16]], ALU.not_equal, 65536, 0, 0)
-        inblock(R("BO"), R("ONEB", C(0, 128)))
-        sel(R("IZ"), R("ONEB", C(0, 224)), [[-1, 224]], ALU.is_equal, 0, 96)
-
-    def constants_d():
-        sel(R("CIND"), R("ONEB", C(0, 64)), [[-2, 64]], ALU.is_ge, 0, 0)
-        sel(R("CIND"), R("CIND"), [[2, 64]], ALU.is_ge, 0, 1, -1)
-        sel(R("UN"), R("ZER"), [[1, 128]], ALU.is_ge, -1, 0, -1)
-        sel(R("UN"), R("UN"), nblk, ALU.is_ge, 0, 15, -1)
-        sel(R("BA", (0, 16)), R("ONEB", (0, 16), C(0, 128)), [[0, 8], [-1, 16]], ALU.is_equal, 0, 0)
-        iota(R("BB", (0, 16)), [[0, 256]], 81920)
-        sel(R("BB", (0, 16)), R("BB", (0, 16)), [[0, 16], [-1, 16]], ALU.not_equal, 16384, 0)
-        iota(R("D2"), [[0, 256]], -1000000)
-        iota(R("SIG"), [[1, 64]], 1)
-        for q in range(4):
-            sel(R("PQ", W(128 * q, 128)), R("ONEB", C(0, 128)), [[0, 4], [-1, 32]], ALU.is_equal, 0, -32 * q)
-        i = R("ZER")
-        for k, v in ((0, -16), (1, 16), (-15, -16)):
-            sel(R("THM"), i, [[-1, 128]], ALU.not_equal, v, -k)
-            i = R("THM")
-        inblock(i, i)
-        sel(R("IWR"), R("ONE"), [[0, 2], [-1, 128]], ALU.is_equal, 0, 0)
-        sel(R("QL"), R("ZER", C(0, 64)), [[-32, 4], [-1, 16]], ALU.not_equal, 1, 0)
-        sel(R("QL"), R("QL"), [[-32, 4], [-1, 16]], ALU.not_equal, 1, -16)
-        iota(R("HW"), [[0, 2]], 15)
-        for a in (0, 64):
-            sel(R("HW", (a, a + 64)), R("HW", (a, a + 64)), [[-8, 2]], ALU.is_ge, 0, -16 * d)
-            sel(R("HW", (a, a + 64)), R("HW", (a, a + 64)), [[8, 2]], ALU.is_ge, 0, 16 * d + 7, -1)
-
-    def constants_c():
-        lin(cf(SG4, 4), R("ROW", C(0, 4)), 16.0, cf(LH))
-        lin(R("DD"), R("ZER"))
-        for a in (0, 128):
-            lin(R("BOW", W(a, 128)), R("BO"))
-        for j in range(4):
-            lin(R("DD", (32 * j, 32 * j + 32), W(32 * j, 32)), R("DM", (32 * j, 32 * j + 32), W(32 * ((j + 1) % 4), 32)), -1.0)
-        for q in range(4):
-            lin(R("BQ", W(128 * q, 128)), R("SH"), cf(JQ + q))
-        lin(R("MO"), R("BO"), cf(CM))
+        ts(R("DM", W(32 * j, 32)), R("DMF"), cf(NJ + j), ALU.mult)
+    ts(R("TIE", (0, 32)), R("DMF", (0, 32), C(0, 32)), 8.0, ALU.mult)
+    ts(R("TIE", (64, 96)), R("SH", (64, 96)), R("CF", (64, 96), W(E01 + 1, 1)), ALU.mult)
+    ts(R("TIE", (32, 64)), R("SH", (32, 64)), R("CF", (32, 64), W(ED, 1)), ALU.mult, 496.0, ALU.mult)
+    copy(slot("WB")(d), R("W32"))
+    copy(R("IF"), R("INC32"))
+    for s in others:
+        copy(slot("PU")(s), slot("PIN32")(s))
+    send("apin", slot("PU"), slot("PINU"))
+    send("aw", lambda s: slot("WB")(d), slot("WB"))
 
     def lists_make(t, bank):
         for cx in range(2):
             mm(ps(bank, C(0, 256)), R("PT", W(128 * (2 * t + cx), 128)), R("IF", C(cx, 512, 2)), cx == 0, cx == 1)
 
-    def lists_go(t, bank):
-        lin(R("IWF", W(256 * t, 256)), ps(bank, C(0, 256)), None, -16384.0)
-        name = "DI%d" % t
-        for i in range(4):
-            stage(name, i, R("IWF", W(256 * t + 64 * i, 64)))
-        dma("Y", slot("IW%d" % t, 64)(d), dram(name, d))
-        send("ai%d" % t, lambda s: dram(name, s), slot("IW%d" % t, 64))
+    whole = (0, 0, 0, 127, None)
 
-    def lists_out(t):
-        ts(R("OT%d" % t), R("IW%d" % t), 16384.0, ALU.add)
+    def lists_stage(t, bank):
+        name = "DI%d" % t
+        copy(R("OS", W(256 * t, 256)), ps(bank, C(0, 256)))
+        dmas([("Y", (T[name][:, 32 * i:32 * i + 32, :], name, whole, None), R("OS", W(256 * t + 64 * i, 64))) for i in range(4)])
+        dma("Y", slot("OT%d" % t, 64)(d), (T[name][d], name, whole, None))
+
+    def lists_send(t):
+        send("ai%d" % t, lambda s: (T["DI%d" % t][s], "DI%d" % t, whole, None), slot("OT%d" % t, 64))
+
+    def constants_r(step):
+        if step == 0:
+            for k in range(2):
+                lin(cf(DS + k), cf(NJ + 2 + k), -1.0, cf(NJ + k))
+            lin(cf(DB), cf(LAM), -1.0, TOP - 8192)
+            lin(cf(RB), cf(LAM), -1.0, -159.0)
+            lin(cf(CB), cf(JJ), 64.0)
+            lin(R("BON"), R("BO"), -128.0)
+            for j in range(4):
+                lin(R("BQ", W(128 * j + 96, 32)), R("BO", W(32 * j, 32)))
+            lin(R("D2", C(0, 256, 16)), R("ROW"), -16.0, cf(DB))
+            for a in range(0, 128, 32):
+                lin(R("DLH", W(a, 32)), R("DMF"), cf(DS))
+        elif step == 1:
+            for a in (0, 128):
+                lin(R("BOW", W(a, 128)), R("BO"))
+        else:
+            for a in range(128, 256, 32):
+                lin(R("DLH", W(a, 32)), R("DMF"), cf(DS + 1))
+
+    def constants_g(step):
+        one = R("ONEB", C(0, 128))
+        if step == 1:
+            sel(R("CC", C(0, 64)), R("CC", C(64, 128)), [[-2, 64]], ALU.is_ge, 0, 0)
+            sel(R("UN"), R("UN"), [[16, 8], [0, 16]], ALU.is_ge, 0, 15, -1)
+            iota(R("MC", (0, 16)), [[2048, 4], [0, 64]], 128, 128)
+            sel(R("UN"), R("UN"), [[1, 128]], ALU.not_equal, -128, 0, -1)
+            lists_send(0)
+            iota(R("BQ"), [[0, 608]], 0)
+            iota(R("D2"), [[0, 256]], 1000000)
+            iota(R("ZNO", C(64, 240)), [[0, 176]], 0)
+            iota(R("BB", (0, 16)), [[0, 128]], -65536)
+            sel(R("IZ"), R("ONEB"), [[-1, 224]], ALU.is_equal, 0, 96)
+            sel(R("IS"), R("ZER"), [[-1, 128]], ALU.not_equal, -16, 0)
+            sel(R("BB", (0, 16)), R("BB", (0, 16)), [[0, 8], [-1, 16]], ALU.not_equal, 0, 0)
+            iota(R("RC"), [[0, 4], [1, 64]], 0)
+            for q in range(4):
+                sel(R("PQ", W(128 * q, 128)), one, [[0, 4], [-1, 32]], ALU.is_equal, 0, -32 * q)
+            iota(R("SIG"), [[1, 64]], -127)
+            sel(R("IWR"), R("IWR"), [[0, 2], [-1, 128]], ALU.is_equal, 0, 0)
+            iota(R("S", C(8192, TW)), [[0, 256]], 0)
+            return
+        iota(R("IWR"), [[0, 256]], 1)
+        iota(R("ONEB"), [[0, 224]], 1)
+        perms(0)
+        iota(R("D0"), [[0, 256]], -16)
+        perms(1)
+        sel(R("D0"), R("D0"), [[0, 16], [1, 16]], ALU.not_equal, 65536, 0, 0)
+        sel(R("BO"), one, [[-16, 8], [0, 16]], ALU.is_ge, 0, 0)
+        iota(R("ZER"), [[0, 128]], 0)
+        sel(R("BO"), R("BO"), [[16, 8], [0, 16]], ALU.is_ge, 0, 15, -1)
+        sel(R("BA", (0, 16)), R("ONEB", (0, 16), C(0, 128)), [[0, 8], [-1, 16]], ALU.is_equal, 0, 0)
+        sel(R("CC", C(64, 128)), R("ONEB", C(0, 64)), [[2, 64]], ALU.is_ge, 0, 1, -1)
+        sel(R("UN"), R("ZER"), [[1, 128]], ALU.is_ge, -1, 0, -1)
+
+    def constants_late():
+        lists_send(1)
+        for name, v in (("IP", 32), ("IM", -32)):
+            sel(R(name), R("ZER"), [[-1, 128]], ALU.not_equal, v, 0)
+        sel(R("QL"), R("ZER", C(0, 64)), [[-32, 4], [-1, 16]], ALU.not_equal, 1, 0)
+        iota(R("CSW"), [[0, 224]], 0)
+        sel(R("QL"), R("QL"), [[-32, 4], [-1, 16]], ALU.not_equal, 1, -16)
+        iota(R("M", C(0, 528)), [[0, 528]], 0)
+        dmas([("Y", R("M", W(528 * a, 528)), R("M", C(0, 528))) for a in range(1, 16)])
+        iota(R("HW"), [[0, 2]], 15)
+        for a in (0, 64):
+            sel(R("HW", (a, a + 64)), R("HW", (a, a + 64)), [[-8, 2]], ALU.is_ge, 0, -16 * d)
+            sel(R("HW", (a, a + 64)), R("HW", (a, a + 64)), [[8, 2]], ALU.is_ge, 0, 16 * d + 7, -1)
+        iota(R("CUTS"), [[0, 4]], 0)
 
     def spread(bank, name, s, b, more):
         a = 64 * (b // 2)
@@ -330,226 +352,252 @@ def rank_program(g, core, T, topo):
             mm(ps(bank, W(128 * x, 128)), R("SEL", (a, a + 64), W(128 * (4 * (b % 2) + x), 128)),
                R(name, (a, a + 64), W(128 * s, 128)), x == 0 or not more, not more)
 
-    n = 0
-    for s in [d] + others:
-        for b in range(4):
-            bank = n % 7
-            spread(bank, "PB", s, b, False)
-            o = R("WIN", W(2048 * s + 512 * b, 512))
-            if n in (4, 6, 8, 10, 12, 14):
-                ts(o, ps(bank), cf(RAMP), ALU.add, 0.0, ALU.max)
-            else:
-                act(o, ps(bank), ACT.Relu, bias=cf(RAMP))
-            if n == 3:
-                send("apin", lambda s: dram("DP", s), slot("PINU"))
-                constants_a()
-                lists_make(0, 7)
-                lists_go(0, 7)
-                constants_b()
-            n += 1
+    pieces = [(d, 0, 2, 0, "S"), (d, 2, 2, 2, "S")]
+    pieces += [(s, b, 1, (4 + 4 * j + b) % 8, "SV"[b % 2]) for j, s in enumerate(others) for b in range(4)]
+    for k, (s, b, n, bank, q) in enumerate(pieces):
+        for x in range(n):
+            spread(bank + x, "PB", s, b + x, False)
+        o = R("WIN", W(2048 * s + 512 * b, 512 * n))
+        if q == "V":
+            ts(o, ps(bank, C(0, 512 * n)), cf(RAMP), ALU.add, 0.0, ALU.max)
+        else:
+            act(o, ps(bank, C(0, 512 * n)), ACT.Relu, bias=cf(RAMP))
+        if k == 1:
+            ts(cf(MX, 2), R("ROW", C(0, 2)), cf(XX), ALU.is_equal)
+            ts(cf(MH, 2), R("ROW", C(0, 2)), cf(HH), ALU.is_equal)
+            copy(slot("PINU")(d), slot("PIN32")(d))
+    constants_g(0)
 
-    chunks = [4 * s + b for s in [d] + others for b in range(4)]
-    chunks = [chunks[k] for k in (0, 1, 2, 4, 3, 5, 6, 8, 7, 9, 10, 12, 11, 13, 14, 15)]
-    banks = [0, 1, 2, 3, 4, 5, 7, 0, 1, 2, 3, 4, 5, 7, 1, 2]
+    halves = [2 * s + a for s in [d] + others for a in range(2)]
     LAG = 4
 
+    def weights(k):
+        for x in range(2):
+            spread(2 * (k % 4) + x, "WB", halves[k] // 2, 2 * (halves[k] % 2) + x, True)
+
     def gath(k):
-        ch = chunks[k]
-        n = 1 if k < 2 or k >= 14 else 2 if k % 4 >= 2 else 0
-        src = IND(R("WIN"), R("PINU", W(32 * ch, 32 * max(n, 1))))
-        spread(banks[k], "WB", ch // 4, ch % 4, True)
-        if n and k % 2 == 0:
-            copy(R("G", W(512 * ch, 512 * n)), src)
-        elif n:
-            act(R("G", W(512 * ch, 512 * n)), src, ACT.Copy)
-        mm(ps(banks[k]), R("DM"), R("G", W(512 * ch, 512)), False, True)
+        a = 1024 * halves[k]
+        src = IND(R("WIN"), R("PINU", W(a // 16, 64)))
+        if k % 2 == 0:
+            copy(R("G", W(a, 1024)), src)
+        else:
+            act(R("G", W(a, 1024)), src, ACT.Copy)
+        for x in range(2):
+            mm(ps(2 * (k % 4) + x), R("DM"), R("G", W(a + 512 * x, 512)), False, True)
 
     def evac(k):
-        o = R("S", W(512 * chunks[k], 512))
+        o = R("S", W(1024 * halves[k], 1024))
         if k % 2 == 0:
-            copy(o, ps(banks[k]))
+            copy(o, ps(2 * (k % 4), C(0, 1024)))
         else:
-            act(o, ps(banks[k]), ACT.Copy)
+            act(o, ps(2 * (k % 4), C(0, 1024)), ACT.Copy)
 
     def keys(q, l): return ps(5 if q == 3 and l >= 4 else q, W(32 * l, 32))
 
     def ties(t, q):
         for l in range(8):
-            mm(keys(q, l), R("WIN", C(2048 * q + 2 * l + t, 2048 * q + 2048, 16)), R("TIE"), l == 0 or (q, l) == (3, 4), False)
+            mm(keys(q, l), R("WIN", (0, 96), C(2048 * q + 2 * l + t, 2048 * q + 2048, 16)), R("TIE", (0, 96)),
+               l == 0 or (q, l) == (3, 4), False)
 
-    for k in range(16):
+    for k in range(2):
+        weights(k)
+    lists_make(0, 7)
+    for k in range(0, 8 + LAG, 2):
+        for x in (k, k + 1):
+            if k >= LAG:
+                evac(x - LAG)
+        for x in (k, k + 1):
+            if LAG <= k < 8:
+                weights(x)
+        for x in (k + 1, k):
+            if k < 8:
+                gath(x)
         if k == 0:
-            lists_make(1, 6)
-        if k == 2:
-            lists_go(1, 6)
-            constants_d()
-        gath(k)
-        if k >= LAG:
-            evac(k - LAG)
-        if k == 5:
-            lin(R("TIE", (0, 32)), R("DM", (0, 32), C(32, 64)), 8.0)
-        if k == 12:
-            lists_out(0)
-    ties(0, 0)
-    for k in range(16 - LAG, 16):
-        evac(k)
+            lists_stage(0, 7)
+            constants_g(1)
+            weights(2)
+            weights(3)
+        if k == 8:
+            ties(0, 0)
+    lists_make(1, 6)
 
     def spare(a, n): return R("G", W(a, n))
 
-    def cutmm(b, bank, zs):
-        for z in zs:
-            mm(ps(bank), R("CSW", W(96 - 32 * z, 128)), R("S", W(2048 * z + 512 * b, 512)), z == 0, z == 3)
+    CUTB = (4, 6, 7, 1)
+    todo = [(b, z) for b in range(4) for z in range(4)]
+
+    def cutsome(t, n):
+        for _ in range(n * t):
+            b, z = todo.pop(0)
+            mm(ps(CUTB[b]), R("CSW", W(96 - 32 * z, 128)), R("S", W(2048 * z + 512 * b, 512)), z == 0, z == 3)
 
     def cutev(b, bank):
         act(spare(512 * b, 512), ps(bank), ACT.Relu, acc=R("CACC", W(b, 1)))
 
     def newparts(t, step):
+        bank = (7, 5)[t]
         if step == 0:
-            lin(R("NB"), R("YB", C(0, 64)), 1.0 / 16, 160 - 7.5 / 16)
-            act(R("NA"), R("ZB", C(0, 64)), ACT.Abs, bias=-32.5)
-            act(R("SG"), R("NA"), ACT.Sign, bias=32.0, scale=-1.0)
+            act(R("SG"), zno(0, 64), ACT.Sign, bias=-63.5, scale=-1.0)
         elif step == 1:
-            mm(ps(4, W(128, 64)), ID, R("NB"), True, False)
-            mm(ps(4, W(128, 64)), R("IP"), R("SG"), False, True)
-            mm(ps(4, W(192, 64)), ID, R("YB", C(0, 64)), True, False)
-            mm(ps(4, W(192, 64)), R("IS"), R("NB"), False, False)
-            mm(ps(4, W(192, 64)), R("IM"), R("SG"), False, True)
+            for k, m in enumerate(("IP", "IM")):
+                mm(ps(bank, W(128 + 64 * k, 64)), ID, zno(1 + k, 64), True, False)
+                mm(ps(bank, W(128 + 64 * k, 64)), R(m), R("SG"), False, True)
         elif step == 2:
-            for k in range(2):
-                for h in range(2):
-                    act(R("LN", W(128 * k + 64 * h, 64)), ps(4, W(128 + 64 * k, 64)), ACT.Relu, bias=cf((B1, B2)[k] + h),
-                        scale=cf(MH + h))
+            for h in range(2):
+                if t == 0:
+                    act(R("LN", C(0, 2), h), ps(bank, W(128, 128)), ACT.Relu, bias=cf(B1 + h), scale=cf(MH + h))
+                else:
+                    ts(R("LN", C(0, 2), h), ps(bank, W(128, 128)), cf(MH + h), ALU.mult, 191.0, ALU.max)
         elif step == 3:
             for k in range(2):
-                mm(ps(4, W(256, 64)), R("LN", W(128 * k, 128)), R("QL"), k == 0, k == 1)
+                mm(ps(bank, W(256, 64)), R("LN", k), R("QL"), k == 0, k == 1)
+        elif t == 0:
+            lin(R("OUTB", C(0, 4), C(0, 16), t), ps(bank, W(256, 64)), None, -1.0)
         else:
-            lin(R("OUTB", C(0, 4), C(0, 16), t), ps(4, W(256, 64)), None, -1.0)
+            ts(R("OUTB", C(0, 4), C(0, 16), t), ps(bank, W(256, 64)), -1.0 - 4 * 191, ALU.add)
 
-    VC = (28, 28, 26, 30)
+    VC = ((28, 28, 26, 30), (28, 28, 28, 34))
     tab = R("S", C(0, 8192))
 
     for t in range(2):
-        ot = "OT%d" % t
+        def ot(q, a, b): return R("OT%d" % t, C(64 * q + a, 64 * q + b))
         for q in range(4):
-            vc = VC[q]
-            ts(R("GV", W(1024 * q, 16 * vc)), IND(tab, R(ot, W(64 * q, vc))), 0.0, ALU.max)
-            act(R("GV", C(1024 * q + 16 * vc, 1024 * q + 1024)), IND(tab, R(ot, C(64 * q + vc, 64 * q + 64))), ACT.Relu)
+            vc = VC[t][q]
+            ts(R("GV", W(1024 * q, 16 * vc)), IND(tab, ot(q, 0, vc)), 0.0, ALU.max)
+            act(R("GV", C(1024 * q + 16 * vc, 1024 * q + 1024)), IND(tab, ot(q, vc, 64)), ACT.Relu)
             if q > 0:
                 scan(R("SC", W(256 * q - 256, 256)), R("D0"), ps(q - 1, C(0, 256)), 0.0, ALU.add, ALU.min)
-            if t == 1:
-                cutmm(q // 2, 6 + q // 2, [2 * (q % 2), 2 * (q % 2) + 1])
+            if q == 0:
+                cutsome(t, 4)
             for l in range(8):
                 mm(keys(q, l), R("GV", C(1024 * q + l, 1024 * q + 1024, 8)), R("SUMR"), False, l == 7 or (q, l) == (3, 3))
+            cutsome(t, 2 if q < 3 else 3)
             if t == 0 and q < 3:
                 ties(0, q + 1)
         if t == 0:
-            ts(R("SH"), R("SH"), cf(HH), ALU.is_equal)
-            ts(R("D2", C(0, 256, 16)), R("ROW2"), 16.0, ALU.mult, cf(LAM), ALU.add)
+            lists_stage(1, 6)
         for a in range(2):
             scan(R("SC", W(768 + 128 * a, 128)), R("D0", C(0, 128)), ps(3 + 2 * a, W(128 * a, 128)), 0.0, ALU.add, ALU.min)
         if t == 1:
-            cutev(0, 6)
-            cutev(1, 7)
-            cutmm(2, 1, [0, 1, 2, 3])
-            cutev(2, 1)
+            cutev(0, CUTB[0])
+            cutev(1, CUTB[1])
         else:
-            constants_c()
+            constants_r(0)
+            constants_late()
+        mm(ps(2, C(0, 256)), R("BA", (0, 16)), R("MC", (0, 16)), True, False)
         for h in range(2):
             ts(R("YI", C(0, 4), h), R("SC", C(16 * h + 15, 1024, 32)), 511, ALU.bitwise_and)
         for x in range(2):
-            ts(R("L", C(0, 8), x), R("YI"), 256.0, ALU.subtract, cf(MX + x), ALU.mult)
-        mm(ps(4, C(0, 64)), R("L"), R("CIND"))
-        if t == 0:
-            memset(R("CSW"), 0.0)
-        ts(R("FL"), ps(4, C(0, 64)), 0.0, ALU.is_ge)
-        copy(R("YB", C(0, 64)), ps(4, C(0, 64)))
-        mm(ps(5, C(0, 64)), R("BO"), R("FL"))
-        mm(ps(5, C(64, 128)), R("UN"), R("FL"))
-        mm(ps(0, C(0, 256)), R("BA", (0, 16)), R("BB", (0, 16)), True, False)
-        if t == 1:
-            cutmm(3, 6, [0, 1, 2, 3])
-        scan(R("TC"), R("ONE", C(0, 64)), ps(5, C(0, 64)), 0.0, ALU.mult, ALU.add)
+            ts(R("LF", C(0, 8), x), R("YI"), 256.0, ALU.is_ge, cf(MX + x), ALU.mult)
+        mm(ps(4, C(0, 128)), R("LF"), R("CC"))
+        for x in range(2):
+            ts(R("LY", C(0, 8), x), R("YI"), 256.0, ALU.subtract, cf(MX + x), ALU.mult)
+        mm(ps(0, C(0, 64)), R("LY"), R("CC", C(0, 64)))
+        cutsome(t, 1)
+        copy(R("FP"), ps(4, C(0, 128)))
+        lin(zno(1, 64), ps(0, C(0, 64)), 1.0 / 16, 160 - 7.5 / 16)
+        act(R("YB"), ps(0, C(0, 64)), ACT.Copy)
         for x in range(4):
-            act(spare(3072 + 256 * t + 64 * x, 64), R("TC"), ACT.Sign, bias=cf(SG4 + x), scale=-1.0, acc=R("ACC", W(x, 1)))
-        tt(R("CUM"), R("TC"), ps(5, C(64, 128)), ALU.add)
-        tt(R("ZB", C(0, 64)), R("CUM"), R("FL"), ALU.mult)
-        ts(R("OFQ"), R("ACC"), 64.0, ALU.add, 0.5, ALU.mult)
-        ts(R("COLB"), R("ACC"), 62.0, ALU.min, cf(CB), ALU.add)
-        tt(R("EQ"), IND(R("ZB"), R("OFQ")), R("SIG"), ALU.is_equal)
-        for q in range(4):
-            mm(ps(5, W(128 + 4 * q, 4)), R("PQ", W(128 * q, 128)), R("COLB"))
-        for q in range(4):
-            mm(ps((7, 1)[q // 2], W(64 * q, 64)), R("PQ", W(128 * q, 128)), R("EQ"))
+            mm(ps(2, W(64 * x, 64)), R("BON"), R("FP", C(64, 128)), False, x == 3)
+        mm(ps(3, C(0, 64)), R("BO"), R("FP", C(64, 128)), True, False)
+        mm(ps(3, C(0, 64)), R("UN"), R("FP", C(0, 64)), False, True)
+        mm(ps(0, C(64, 128)), ID, R("YB"), True, False)
+        mm(ps(0, C(64, 128)), R("IS"), zno(1, 64), False, True)
+        for a in range(2):
+            mm(ps(4 + 2 * a, C(256, 384)), R("BA", (0, 16)), R("BB", (0, 16), C(0, 128)), True, False)
+        cutsome(t, 2)
+        ts(R("IW"), ot(0, 0, 256), -1.0, ALU.mult, TOP, ALU.add)
+        scan(R("SC3"), R("RC"), ps(2, C(0, 256)), 0.0, ALU.min, ALU.max)
+        act(zno(0, 64), ps(3, C(0, 64)), ACT.Copy)
+        lin(zno(2, 64), ps(0, C(64, 128)), None, 2720.0)
         if t == 1:
             newparts(1, 0)
+            cutev(2, CUTB[2])
         else:
-            act(spare(2048, 512), R("WB"), ACT.Identity, acc=R("WS", C(0, 1)))
-        tt(R("EY"), IND(R("YB"), R("OFQ")), R("EQ"), ALU.mult)
-        act(R("E", C(128, 256)), ps(1, C(128, 256)), ACT.Copy)
-        ts(R("OFC"), ps(5, C(128, 144)), 0.5, ALU.mult)
-        copy(R("E", C(0, 128)), ps(7, C(0, 128)))
-        for bank in (2, 3):
+            constants_r(1)
+        cols = R("SC3", C(63, 256, 64))
+        ts(R("COLB"), cols, 63.0, ALU.min, cf(CB), ALU.add)
+        ts(R("OFQ"), cols, 64.0, ALU.min)
+        tt(R("EQ"), IND(zno(0), R("OFQ")), R("SIG"), ALU.is_equal)
+        for q in range(4):
+            mm(ps(5, W(4 * q, 4)), R("PQ", W(128 * q, 128)), R("COLB"))
+        for q in range(4):
+            mm(ps(3, W(128 + 64 * q, 64)), R("PQ", W(128 * q, 128)), R("EQ"))
+        copy(R("OFC"), ps(5, C(0, 16)))
+        tt(R("EN"), IND(zno(1), R("OFQ")), R("EQ"), ALU.mult)
+        act(R("E", C(128, 256)), IND(R("IW"), R("OFC", W(8, 8))), ACT.Copy)
+
+        def parts(on):
+            if on == 0:
+                tt(R("EO"), IND(zno(2), R("OFQ")), R("EQ"), ALU.mult)
             for q in range(4):
-                mm(ps(bank, W(64 * q, 64)), R("BQ", W(128 * q, 128)), R("EY"), bank == 2 or q == 0, bank == 2)
+                mm(ps(0, W(128 + 64 * (q % 2), 64)), bq(q, 2 * on + q // 2), R(("EO", "EN")[on]), on == 1 and q == 0,
+                   on == 0 and q == 3)
+            if on == 0:
+                act(R("RR"), ps(0, C(128, 256)), ACT.Relu, bias=cf(RB))
+
+        def lanes(a):
+            tt(R("EI", W(128 * a, 128)), R("E", W(128 * a, 128)), ps(3, W(128 + 128 * a, 128)), ALU.mult)
+            mm(ps(4 + 2 * a, C(256, 384)), R("BOW", W(32 - 32 * t, 128)), R("EI", W(128 * a, 128)), False, True)
+
+        def change():
+            for a in range(2):
+                mm(ps(2, W(128 * a, 128)), R("DLH", W(128 * a, 128)), R("RR"))
+            act(R("DL"), ps(2, C(0, 256)), ACT.Copy)
+
         if t == 1:
             newparts(1, 1)
-        for a in range(2):
-            tt(R("EI", W(128 * a, 128)), IND(R("IW%d" % t), R("OFC", W(8 * a, 8))), R("E", W(128 * a, 128)), ALU.mult)
-        act(R("TH"), ps(2, C(0, 256)), ACT.Sign, bias=cf(THB))
-        mm(ps(3, C(0, 256)), R("MO"), R("TH"), False, True)
-        for a in range(2):
-            mm(ps(0, W(128 * a, 128)), R("BOW", W(32 - 32 * t, 128)), R("EI", W(128 * a, 128)), False, a == 1)
-        mm(ps(2, C(0, 256)), R("THM"), R("TH"), True, False)
-        if t == 0:
-            memset(R("S", C(8192, TW)), 0.0)
-            lists_out(1)
-        scan(R("SC2"), R("D2"), ps(0, C(0, 256)), -1000000.0, ALU.max, ALU.min)
-        act(R("RO"), ps(3, C(0, 256)), ACT.Relu, bias=cf(RAMP))
+        else:
+            constants_r(2)
+        parts(1)
+        parts(0)
+        copy(R("E", C(0, 128)), IND(R("IW"), R("OFC", W(0, 8))))
+        lanes(0)
+        change()
+        lanes(1)
         if t == 1:
+            cutev(3, CUTB[3])
             newparts(1, 2)
+            newparts(1, 3)
+        for a in range(2):
+            scan(R("SC2", W(128 * a, 128)), R("D2", W(128 * a, 128)), ps(4 + 2 * a, C(256, 384)), 1000000.0, ALU.min, ALU.max)
         ends = R("SC2", C(15, 256, 16))
-        copy(R("OF", C(0, 16)), ends)
-        mm(ps(2, C(0, 256)), R("DD"), R("RO"), False, True)
+
+        def offs(o, i): ts(o, i, -1.0, ALU.mult, TOP, ALU.add)
+        offs(R("OF", C(0, 16)), ends)
         for k in range(2 + t):
-            mm(ps(1, W(16 * k, 16)), R("IWR", W(32 * k + 32, 128)), ends)
-        act(R("DL"), ps(2, C(0, 256)), ACT.Copy)
+            mm(ps(3, W(16 * k, 16)), R("IWR", W(32 * k + 32, 128)), ends)
         if t == 0:
             for k in range(3):
                 off = R("OF", W(16 * k, 16))
                 copy(R("TMP", C(0, 128)), IND(R("S"), R("OF", W(16 * k, 8))))
                 act(R("TMP", C(128, 256)), IND(R("S"), R("OF", W(16 * k + 8, 8))), ACT.Copy)
                 if k == 0:
-                    copy(R("OF", C(16, 48)), ps(1, C(0, 32)))
-                if k == 1:
-                    ts(R("CSW", C(96, 128)), R("X", C(0, 32)), 0.0, ALU.is_equal)
+                    offs(R("OF", C(16, 48)), ps(3, C(0, 32)))
                 if k == 2:
-                    memset(R("CUTS"), 0.0)
+                    lin(R("CSW", C(96, 128)), R("SUMR"), 1.0 / 512)
+                if k == 2:
                     newparts(0, 4)
-                    lin(R("M", C(0, 704)), R("WIN", C(0, 704)), 0.0)
-                    for a in range(1, 12):
-                        dma("Y", R("M", W(704 * a, 704)), R("M", C(0, 704)))
                 tt(IND(R("S"), off), R("TMP"), R("DL"), ALU.add)
                 if k == 0:
-                    for name, v in (("IP", 32.0), ("IM", -32.0), ("IS", -16.0)):
-                        lin(R(name), ID, v)
                     newparts(0, 0)
                     newparts(0, 1)
+                    for q in range(4):
+                        ties(1, q)
+                if k == 2:
+                    act(spare(2048, 512), R("WB"), ACT.Identity, acc=R("WS", C(0, 1)))
                 if k == 1:
-                    for a, v in ((B1, -191.0), (B2, 2529.0), (HS4, -0.25), (HSM, -1.0)):
+                    for a, v in ((B1, -191.0), (HS4, -0.25), (HSM, -1.0)):
                         lin(cf(a, 2), cf(MH, 2), v)
                     newparts(0, 2)
                     newparts(0, 3)
-                    for q in range(4):
-                        ties(1, q)
         else:
-            copy(IND(R("M"), R("OF", C(0, 16))), R("DL"))
-            newparts(1, 3)
             newparts(1, 4)
             send("anp", lambda s: R("OUTB", s), slot("NPR", 32))
+            copy(IND(R("M"), R("OF", C(0, 16))), R("DL"))
             act(R("TMP"), IND(R("S"), R("OF", C(0, 16))), ACT.Copy)
-            cutev(3, 6)
-            copy(R("OF", C(16, 64)), ps(1, C(0, 48)))
-            sums = ((3, "IM", 0, 128), (0, "IP", 0, 256), (7, "IM", 128, 128))
+            offs(R("OF", C(16, 64)), ps(3, C(0, 48)))
+            sums = ((6, "IM", 0, 128), (0, "IP", 0, 256), (7, "IM", 128, 128))
             for bank, m, a, n in sums:
                 mm(ps(bank, W(a, n)), ID, R("TMP", W(a, n)), True, False)
                 mm(ps(bank, W(a, n)), R(m), R("DL", W(a, n)), False, False)
@@ -557,14 +605,13 @@ def rank_program(g, core, T, topo):
             mm(fin, R("HW"), R("WS", C(0, 1)), True, False)
             for b in range(4):
                 mm(fin, cf(HS4, 2), R("CACC", W(b, 1)), False, False)
-            copy(R("MG", C(0, 256)), IND(R("M"), R("OF", C(16, 32))))
-            act(R("MG", C(512, 768)), IND(R("M"), R("OF", C(48, 64))), ACT.Copy)
-            copy(R("MG", C(256, 384)), IND(R("M"), R("OF", C(32, 40))))
-            act(R("MG", C(384, 512)), IND(R("M"), R("OF", C(40, 48))), ACT.Copy)
-            for k in (1, 3, 2):
-                for bank, m, a, n in sums:
-                    mm(ps(bank, W(a, n)), R("IZ", W(96 - 32 * k, 128)), R("MG", W(256 * k - 256 + a, n)), False, k == 2)
-            ts(R("RL"), ps(3, C(0, 128)), -1024.0, ALU.add, 0.0, ALU.max)
+            for k in (1, 2, 3):
+                copy(R("MG", W(256 * k - 256, 128)), IND(R("M"), R("OF", W(16 * k, 8))))
+                act(R("MG", W(256 * k - 128, 128)), IND(R("M"), R("OF", W(16 * k + 8, 8))), ACT.Copy)
+                for bank, a in ((6, 0), (0, 0), (0, 1), (7, 1)):
+                    mm(ps(bank, W(128 * a, 128)), R("IZ", W(96 - 32 * k, 128)), R("MG", W(256 * k - 256 + 128 * a, 128)),
+                       False, k == 3 and (bank > 0 or a == 1))
+            ts(R("RL"), ps(6, C(0, 128)), -1024.0, ALU.add, 0.0, ALU.max)
             act(spare(2560, 256), ps(0, C(0, 256)), ACT.Relu, bias=-1024.0, acc=R("FD", C(1, 2)))
             act(spare(2816, 128), ps(7, C(128, 256)), ACT.Relu, bias=-1024.0, acc=R("FD", C(2, 3)))
             fd, rl = R("FD", C(0, 1)), R("RL")

from concourse.bass import DstId, RemoteDMATransfer
from concourse.mybir import AluOpType as ALU, AxisListType, ActivationFunctionType as ACT

F32, BF, I32, U16 = "float32", "bfloat16", "int32", "uint16"
TW = 8448
TOP = 16384.0

SCRATCH = {"DI0": ("dram", [4, 128, 64], U16), "DI1": ("dram", [4, 128, 64], U16)}
for _t, _l in (
    (I32, "P32 128,W32 128,PIN32 512,INC32 512,SC 1024,YI 4 2 8,KI 1,CI 4"),
    (U16, "PU 512,PINU 512,OS 512,OT0 256,OT1 256,OFC 16,OFQ 4,OF 64"),
    (F32, "IF 512,IW 256,E 256,SC3 256,EI 256,SC2 256,RL 128,FD 4,CACC 4,WS 4,OUTB 4 16 2,NPR 128,CUTS 4,CUTR 16,CF 40,ROW 16,"
          "PT 512,D0 256,SIG 64,BOW 256,D2 256,IWR 256,HW 2,RC 256"),
    (BF, "PB 512,WB 512,WIN 8192,G 8192,S 8448,M 8448,GV 4096,LF 8 2 8,LY 8 2 8,FP 128,YB 64,ZNO 240,COLB 4,EQ 64,"
         "EN 64,EO 64,RR 128,DL 256,TMP 256,MG 768,SG 64,LN 2 2 64,A 128,SEL 1024,X 32,T1 32,T2 32,T3 32,DM 128,"
         "DMF 32,DLH 256,SUMR 32,TIE 32,CSW 224,ONEB 224,CC 128,BO 128,BON 128,UN 128,PQ 512,BQ 608,SH 32,BA 128,BB 128,"
         "MC 256,QL 64,IZ 224,ZER 128,IP 128,IM 128,IS 128"),
):
    for _e in _l.split(","):
        SCRATCH[_e.split()[0]] = ("sbuf", [128] + [int(_x) for _x in _e.split()[1:]], _t)
for _b in range(4):
    SCRATCH["pp%d" % _b] = ("psum", [128, 1024], F32)
SEMAPHORES = (["eV", "eS", "eP", "sent"] + ["g%d" % k for k in range(1, 61)] + ["dm%d" % k for k in range(32)]
              + ["%s%d" % (m, s) for m in ("ap", "aw", "apin", "ai0", "ai1", "anp", "acut") for s in range(4)])


def rank_program(g, core, T, topo):
    d = T.rank_of(core)
    if d is None:
        return
    Q = {"V": g.vector, "S": g.scalar, "P": g.tensor, "G": g, "Y": g.sync}
    count = {"V": 0, "S": 0, "P": 0, "G": 0}
    seen = {q: {} for q in Q}
    recs = {}
    total = {}
    ndma = [0]
    first = [0]

    def R(name, *idx):
        shape = SCRATCH[name][1][1:]
        part = slice(None)
        if idx and isinstance(idx[0], tuple):
            part = slice(idx[0][0], idx[0][1])
            idx = idx[1:]
        idx = list(idx) + [slice(None)] * (len(shape) - len(idx))
        cols = [0]
        for n, ix in zip(shape, idx):
            r = range(n)[ix] if isinstance(ix, slice) else range(ix, ix + 1)
            cols = [c * n + k for c in cols for k in r]
        rows = range(128)[part]
        gaps = set(cols) if cols[-1] - cols[0] + 1 != len(cols) else None
        return (T[name][tuple([part] + idx)], name, (cols[0], cols[-1], rows[0], rows[-1], gaps), None)

    def meet(a, b):
        if a[1] < b[0] or b[1] < a[0] or a[3] < b[2] or b[3] < a[2]:
            return False
        return a[4] is None or b[4] is None or not a[4].isdisjoint(b[4])

    def C(a, b, step=None): return slice(a, b, step)
    def W(a, n): return slice(a, a + n)
    def IND(win, off): return (win[0].indirect(off[0]), win[1], win[2], off)

    def wait(q, sem, n):
        if seen[q].get(sem, 0) < n:
            Q[q].wait_ge(T.sem[sem], n)
            seen[q][sem] = n

    def order(q, outs, ins, dma=False):
        need = {}
        ins = list(ins)
        for x in outs + ins[:]:
            if x[3] is not None:
                ins.append(x[3])
        for wr, lst in ((True, outs), (False, ins)):
            for x in lst:
                bank = x[1].startswith("ps")
                for (span, w, ev, eq) in recs.get(x[1], []):
                    same = eq == q and not dma
                    if bank and (q == "P" or not same):
                        hit = not same
                    else:
                        hit = (wr or w) and meet(span, x[2])
                    if hit:
                        need[ev[0]] = max(need.get(ev[0], 0), ev[1])
        for s, n in need.items():
            wait(q, s, n)
        return ins

    def note(q, outs, ins, ev):
        for x in outs:
            recs.setdefault(x[1], []).append((x[2], True, ev, q))
        for x in ins:
            recs.setdefault(x[1], []).append((x[2], False, ev, q))
        total[ev[0]] = max(total.get(ev[0], 0), ev[1])

    def ap(x): return x[0] if isinstance(x, tuple) else x

    def emit(q, make, outs, ins):
        ins = order(q, outs, [x for x in ins if isinstance(x, tuple)])
        if q == "G":
            if outs[0][2][2] != first[0]:
                wait("G", "g%d" % count["G"], 1)
            first[0] = outs[0][2][2]
        count[q] += 1
        ev = ("g%d" % count[q], 1) if q == "G" else ("e" + q, count[q])
        make().then_inc(T.sem[ev[0]], 1)
        note(q, outs, ins, ev)

    def copy(o, i): emit("V", lambda: g.vector.tensor_copy(o[0], i[0]), [o], [i])
    def tt(o, a, b, op): emit("V", lambda: g.vector.tensor_tensor(o[0], a[0], b[0], op), [o], [a, b])
    def memset(o, c): emit("V", lambda: g.vector.memset(o[0], c), [o], [])

    def ts(o, a, s1, op0, s2=None, op1=None):
        if op1 is None:
            emit("V", lambda: g.vector.tensor_scalar(o[0], a[0], ap(s1), None, op0), [o], [a, s1])
        else:
            emit("V", lambda: g.vector.tensor_scalar(o[0], a[0], ap(s1), ap(s2), op0, op1), [o], [a, s1, s2])

    def scan(o, a, b, init, op0, op1):
        emit("V", lambda: g.vector.tensor_tensor_scan(o[0], a[0], b[0], init, op0, op1), [o], [a, b])

    def act(o, i, f, bias=None, scale=None, acc=None):
        kw = {}
        if bias is not None: kw["bias"] = ap(bias)
        if scale is not None: kw["scale"] = ap(scale)
        if acc is not None: kw["accum_out"] = acc[0]
        emit("S", lambda: g.scalar.activation(o[0], i[0], f, **kw), [o] + ([acc] if acc else []), [i, bias, scale])

    def lin(o, i, scale=None, bias=None): act(o, i, ACT.Identity, bias=bias, scale=scale)

    def mm(o, l, r, start=True, stop=True):
        emit("P", lambda: g.tensor.matmul(o[0], l[0], r[0], start, stop), [o], [l, r])

    def iota(o, pat, base, cm=0):
        kw = {} if SCRATCH[o[1]][2] == I32 else {"allow_small_or_imprecise_dtypes": True}
        emit("G", lambda: g.iota(o[0], pat, base, cm, **kw), [o], [])

    def sel(o, i, pat, op, fill, base, cm=1):
        emit("G", lambda: g.affine_select(o[0], i[0], pat, op, float(fill), base, cm), [o], [i])

    def dmas(lst):
        s = "dm%d" % ndma[0]
        ndma[0] += 1
        done = []
        for q, o, i in lst:
            outs = [o] if isinstance(o, tuple) else []
            ins = order(q, outs, [i] if isinstance(i, tuple) else [], True)
            Q[q].dma_start(ap(o), ap(i)).then_inc(T.sem[s], 16)
            done.append((outs, ins))
        for outs, ins in done:
            note("D", outs, ins, (s, 16 * len(lst)))

    def dma(q, o, i): dmas([(q, o, i)])

    def load(q, name, src):
        dmas([(q[a], R(name, (64 * a, 64 * a + 64)), src[:, 1024 * a:1024 * a + 1024]) for a in range(2)])

    def load_lists(q, name, src, s):
        dmas([(q[i % len(q)], R(name, (32 * i, 32 * i + 32), W(128 * s, 128)), src[32 * s:32 * s + 32, 128 * i:128 * i + 128])
              for i in range(4)])

    def masks(r):
        me = T.cores[r]
        far = [s for s in range(4) if T.cores[s] not in topo.cores_of(me)]
        used, out = [], {}
        for k, s in enumerate(far):
            e = topo.engines(me, T.cores[s])
            n = len(e) // len(far)
            out[s] = e[k * n:(k + 1) * n]
            used += out[s]
        for s in range(4):
            if s != r and s not in far:
                out[s] = [e for e in topo.engines(me, T.cores[s]) if e not in used][:len(used) // 2]
        return out

    mine = masks(d)
    others = sorted(mine, key=lambda s: (T.cores[s] not in topo.cores_of(core), s))
    sent = [0]

    def send(tag, src, dst):
        srcs = [src(s) for s in others]
        order("G", [], srcs, True)
        trs = []
        for s, x in zip(others, srcs):
            rid, pid = topo.addr(T.cores[s], core)
            trs.append(RemoteDMATransfer(dst_ids=[DstId(rid=rid, pnc=pid)], dma_engine_mask=sum(1 << e for e in mine[s]),
                                         remote_sem=T.sem["%s%d" % (tag, d)], src=x[0], dst=dst(d)[0]))
            sent[0] += len(mine[s])
        g.remote_dma_fused(trs, local_sem=T.sem.sent)
        total["sent"] = sent[0]
        for s in others:
            note("D", [dst(s)], [], ("%s%d" % (tag, s), len(masks(s)[d])))

    def slot(name, n=128): return lambda s: R(name, W(n * s, n))

    def ps(b, *idx):
        p = idx[0] if idx and isinstance(idx[0], tuple) else (0, 128)
        c = idx[-1] if idx and isinstance(idx[-1], slice) else C(0, 512)
        a = 512 * (b % 2)
        more = (None, "ps%d" % (b + 1), (0, c.stop - 513, p[0], p[1] - 1, None), None) if c.stop > 512 else None
        return (T["pp%d" % (b // 2)][p[0]:p[1], a + c.start:a + c.stop], "ps%d" % b,
                (c.start, min(c.stop, 512) - 1, p[0], p[1] - 1, None), more)

    def cf(k, n=1): return R("CF", W(k, n))
    LAM, HH, JJ, XX, RAMP, CX, K64, AH, RB, CB, MX, MH, JQ, HS4, HSM, B1, E01, ED, DS, KF, DB, NJ = (
        0, 1, 2, 3, 4, 5, 6, 7, 8, 9, 10, 12, 14, 18, 20, 22, 24, 26, 27, 29, 30, 32)
    ID = R("IZ", C(96, 224))
    def bq(q, blk): return R("BQ", W(128 * q + 96 - 32 * blk, 128))
    def zno(k, n=80): return R("ZNO", W(80 * k, n))

    load("YS", "P32", T.part)
    load("YS", "W32", T.w)
    dma("S", R("INC32"), T.inc[:])
    for s in others:
        load_lists("YYYS", "PIN32", T.pin, s)
    load_lists("Y", "PIN32", T.pin, d)
    iota(R("KI"), [[0, 1]], 0, 1)
    iota(R("A"), [[0, 4], [-8, 2], [0, 16]], -16 * d, 1)
    iota(R("X"), [[-100, 2], [-1, 16]], 0)
    ts(cf(K64), R("KI"), 64.0, ALU.is_ge, 64.0, ALU.mult)
    ts(R("CI", C(0, 1)), R("KI"), 15, ALU.bitwise_and)
    ts(R("CI", C(1, 2)), R("KI"), 4, ALU.logical_shift_right, 1, ALU.bitwise_and)
    ts(R("CI", C(2, 3)), R("KI"), 5, ALU.logical_shift_right)
    ts(R("CI", C(3, 4)), R("KI"), 1, ALU.bitwise_and)
    copy(cf(KF), R("KI"))
    copy(cf(0, 4), R("CI"))
    lin(cf(RAMP), cf(LAM), -1.0, 1.0)
    lin(cf(CX), cf(HH), 100.0, cf(LAM))
    lin(R("ROW"), R("X", C(0, 16)), -1.0)
    lin(R("X"), R("X"), None, cf(CX))
    lin(cf(AH), cf(HH), -8.0, cf(KF))
    for c in range(8):
        ts(R("SEL", W(128 * c, 128)), R("A"), cf(K64), ALU.subtract, float(c), ALU.is_equal)
    copy(slot("PB")(d), R("P32"))
    send("ap", lambda s: slot("PB")(d), slot("PB"))

    def perms(t):
        for cx in range(2):
            sel(R("PT", W(128 * (2 * t + cx), 128)), R("IWR", C(0, 128)), [[-16, 8], [-1000, 2], [-2, 8]], ALU.is_equal, 0,
                1000 * cx - t)

    ts(R("T1"), R("X"), 0.0, ALU.is_equal, -32.0, ALU.mult)
    ts(R("T2"), R("X"), 1.0, ALU.is_equal, 64.0, ALU.mult)
    ts(R("T3"), R("X"), 2.0, ALU.is_equal, -32.0, ALU.mult)
    ts(cf(NJ, 4), R("ROW", C(0, 4)), cf(JJ), ALU.not_equal)
    tt(R("T1"), R("T1"), R("T2"), ALU.add)
    ts(cf(E01, 2), R("ROW", C(0, 2)), cf(LAM), ALU.is_equal)
    ts(R("SH"), R("A", C(0, 32)), float(16 * d), ALU.add, cf(AH), ALU.is_equal)
    tt(R("DMF"), R("T1"), R("T3"), ALU.add)
    ts(R("SUMR"), R("X", C(0, 32)), 0.0, ALU.is_equal, 512.0, ALU.mult)
    tt(cf(ED), cf(E01), cf(E01 + 1), ALU.subtract)
    for j in range(4):
        ts(R("DM", W(32 * j, 32)), R("DMF"), cf(NJ + j), ALU.mult)
    ts(R("TIE", (0, 32)), R("DMF", (0, 32), C(0, 32)), 8.0, ALU.mult)
    ts(R("TIE", (64, 96)), R("SH", (64, 96)), R("CF", (64, 96), W(E01 + 1, 1)), ALU.mult)
    ts(R("TIE", (32, 64)), R("SH", (32, 64)), R("CF", (32, 64), W(ED, 1)), ALU.mult, 496.0, ALU.mult)
    copy(slot("WB")(d), R("W32"))
    copy(R("IF"), R("INC32"))
    for s in others:
        copy(slot("PU")(s), slot("PIN32")(s))
    send("apin", slot("PU"), slot("PINU"))
    send("aw", lambda s: slot("WB")(d), slot("WB"))

    def lists_make(t, bank):
        for cx in range(2):
            mm(ps(bank, C(0, 256)), R("PT", W(128 * (2 * t + cx), 128)), R("IF", C(cx, 512, 2)), cx == 0, cx == 1)

    whole = (0, 0, 0, 127, None)

    def lists_stage(t, bank):
        name = "DI%d" % t
        copy(R("OS", W(256 * t, 256)), ps(bank, C(0, 256)))
        dmas([("Y", (T[name][:, 32 * i:32 * i + 32, :], name, whole, None), R("OS", W(256 * t + 64 * i, 64))) for i in range(4)])
        dma("Y", slot("OT%d" % t, 64)(d), (T[name][d], name, whole, None))

    def lists_send(t):
        send("ai%d" % t, lambda s: (T["DI%d" % t][s], "DI%d" % t, whole, None), slot("OT%d" % t, 64))

    def constants_r(step):
        if step == 0:
            for k in range(2):
                lin(cf(DS + k), cf(NJ + 2 + k), -1.0, cf(NJ + k))
            lin(cf(DB), cf(LAM), -1.0, TOP - 8192)
            lin(cf(RB), cf(LAM), -1.0, -159.0)
            lin(cf(CB), cf(JJ), 64.0)
            lin(R("BON"), R("BO"), -128.0)
            for j in range(4):
                lin(R("BQ", W(128 * j + 96, 32)), R("BO", W(32 * j, 32)))
            lin(R("D2", C(0, 256, 16)), R("ROW"), -16.0, cf(DB))
            for a in range(0, 128, 32):
                lin(R("DLH", W(a, 32)), R("DMF"), cf(DS))
        elif step == 1:
            for a in (0, 128):
                lin(R("BOW", W(a, 128)), R("BO"))
        else:
            for a in range(128, 256, 32):
                lin(R("DLH", W(a, 32)), R("DMF"), cf(DS + 1))

    def constants_g(step):
        one = R("ONEB", C(0, 128))
        if step == 1:
            sel(R("CC", C(0, 64)), R("CC", C(64, 128)), [[-2, 64]], ALU.is_ge, 0, 0)
            sel(R("UN"), R("UN"), [[16, 8], [0, 16]], ALU.is_ge, 0, 15, -1)
            iota(R("MC", (0, 16)), [[2048, 4], [0, 64]], 128, 128)
            sel(R("UN"), R("UN"), [[1, 128]], ALU.not_equal, -128, 0, -1)
            lists_send(0)
            iota(R("BQ"), [[0, 608]], 0)
            iota(R("D2"), [[0, 256]], 1000000)
            iota(R("ZNO", C(64, 240)), [[0, 176]], 0)
            iota(R("BB", (0, 16)), [[0, 128]], -65536)
            sel(R("IZ"), R("ONEB"), [[-1, 224]], ALU.is_equal, 0, 96)
            sel(R("IS"), R("ZER"), [[-1, 128]], ALU.not_equal, -16, 0)
            sel(R("BB", (0, 16)), R("BB", (0, 16)), [[0, 8], [-1, 16]], ALU.not_equal, 0, 0)
            iota(R("RC"), [[0, 4], [1, 64]], 0)
            for q in range(4):
                sel(R("PQ", W(128 * q, 128)), one, [[0, 4], [-1, 32]], ALU.is_equal, 0, -32 * q)
            iota(R("SIG"), [[1, 64]], -127)
            sel(R("IWR"), R("IWR"), [[0, 2], [-1, 128]], ALU.is_equal, 0, 0)
            iota(R("S", C(8192, TW)), [[0, 256]], 0)
            return
        iota(R("IWR"), [[0, 256]], 1)
        iota(R("ONEB"), [[0, 224]], 1)
        perms(0)
        iota(R("D0"), [[0, 256]], -16)
        perms(1)
        sel(R("D0"), R("D0"), [[0, 16], [1, 16]], ALU.not_equal, 65536, 0, 0)
        sel(R("BO"), one, [[-16, 8], [0, 16]], ALU.is_ge, 0, 0)
        iota(R("ZER"), [[0, 128]], 0)
        sel(R("BO"), R("BO"), [[16, 8], [0, 16]], ALU.is_ge, 0, 15, -1)
        sel(R("BA", (0, 16)), R("ONEB", (0, 16), C(0, 128)), [[0, 8], [-1, 16]], ALU.is_equal, 0, 0)
        sel(R("CC", C(64, 128)), R("ONEB", C(0, 64)), [[2, 64]], ALU.is_ge, 0, 1, -1)
        sel(R("UN"), R("ZER"), [[1, 128]], ALU.is_ge, -1, 0, -1)

    def constants_late():
        lists_send(1)
        for name, v in (("IP", 32), ("IM", -32)):
            sel(R(name), R("ZER"), [[-1, 128]], ALU.not_equal, v, 0)
        sel(R("QL"), R("ZER", C(0, 64)), [[-32, 4], [-1, 16]], ALU.not_equal, 1, 0)
        iota(R("CSW"), [[0, 224]], 0)
        sel(R("QL"), R("QL"), [[-32, 4], [-1, 16]], ALU.not_equal, 1, -16)
        iota(R("M", C(0, 528)), [[0, 528]], 0)
        dmas([("Y", R("M", W(528 * a, 528)), R("M", C(0, 528))) for a in range(1, 16)])
        iota(R("HW"), [[0, 2]], 15)
        for a in (0, 64):
            sel(R("HW", (a, a + 64)), R("HW", (a, a + 64)), [[-8, 2]], ALU.is_ge, 0, -16 * d)
            sel(R("HW", (a, a + 64)), R("HW", (a, a + 64)), [[8, 2]], ALU.is_ge, 0, 16 * d + 7, -1)
        iota(R("CUTS"), [[0, 4]], 0)

    def spread(bank, name, s, b, more):
        a = 64 * (b // 2)
        for x in range(4):
            mm(ps(bank, W(128 * x, 128)), R("SEL", (a, a + 64), W(128 * (4 * (b % 2) + x), 128)),
               R(name, (a, a + 64), W(128 * s, 128)), x == 0 or not more, not more)

    pieces = [(d, 0, 2, 0, "S"), (d, 2, 2, 2, "S")]
    pieces += [(s, b, 1, (4 + 4 * j + b) % 8, "SV"[b % 2]) for j, s in enumerate(others) for b in range(4)]
    for k, (s, b, n, bank, q) in enumerate(pieces):
        for x in range(n):
            spread(bank + x, "PB", s, b + x, False)
        o = R("WIN", W(2048 * s + 512 * b, 512 * n))
        if q == "V":
            ts(o, ps(bank, C(0, 512 * n)), cf(RAMP), ALU.add, 0.0, ALU.max)
        else:
            act(o, ps(bank, C(0, 512 * n)), ACT.Relu, bias=cf(RAMP))
        if k == 1:
            ts(cf(MX, 2), R("ROW", C(0, 2)), cf(XX), ALU.is_equal)
            ts(cf(MH, 2), R("ROW", C(0, 2)), cf(HH), ALU.is_equal)
            copy(slot("PINU")(d), slot("PIN32")(d))
    constants_g(0)

    halves = [2 * s + a for s in [d] + others for a in range(2)]
    LAG = 4

    def weights(k):
        for x in range(2):
            spread(2 * (k % 4) + x, "WB", halves[k] // 2, 2 * (halves[k] % 2) + x, True)

    def gath(k):
        a = 1024 * halves[k]
        src = IND(R("WIN"), R("PINU", W(a // 16, 64)))
        if k % 2 == 0:
            copy(R("G", W(a, 1024)), src)
        else:
            act(R("G", W(a, 1024)), src, ACT.Copy)
        for x in range(2):
            mm(ps(2 * (k % 4) + x), R("DM"), R("G", W(a + 512 * x, 512)), False, True)

    def evac(k):
        o = R("S", W(1024 * halves[k], 1024))
        if k % 2 == 0:
            copy(o, ps(2 * (k % 4), C(0, 1024)))
        else:
            act(o, ps(2 * (k % 4), C(0, 1024)), ACT.Copy)

    def keys(q, l): return ps(5 if q == 3 and l >= 4 else q, W(32 * l, 32))

    def ties(t, q):
        for l in range(8):
            mm(keys(q, l), R("WIN", (0, 96), C(2048 * q + 2 * l + t, 2048 * q + 2048, 16)), R("TIE", (0, 96)),
               l == 0 or (q, l) == (3, 4), False)

    for k in range(2):
        weights(k)
    lists_make(0, 7)
    for k in range(0, 8 + LAG, 2):
        for x in (k, k + 1):
            if k >= LAG:
                evac(x - LAG)
        for x in (k, k + 1):
            if LAG <= k < 8:
                weights(x)
        for x in (k + 1, k):
            if k < 8:
                gath(x)
        if k == 0:
            lists_stage(0, 7)
            constants_g(1)
            weights(2)
            weights(3)
        if k == 8:
            ties(0, 0)
    lists_make(1, 6)

    def spare(a, n): return R("G", W(a, n))

    CUTB = (4, 6, 7, 1)
    todo = [(b, z) for b in range(4) for z in range(4)]

    def cutsome(t, n):
        for _ in range(n * t):
            b, z = todo.pop(0)
            mm(ps(CUTB[b]), R("CSW", W(96 - 32 * z, 128)), R("S", W(2048 * z + 512 * b, 512)), z == 0, z == 3)

    def cutev(b, bank):
        act(spare(512 * b, 512), ps(bank), ACT.Relu, acc=R("CACC", W(b, 1)))

    def newparts(t, step):
        bank = (7, 5)[t]
        if step == 0:
            act(R("SG"), zno(0, 64), ACT.Sign, bias=-63.5, scale=-1.0)
        elif step == 1:
            for k, m in enumerate(("IP", "IM")):
                mm(ps(bank, W(128 + 64 * k, 64)), ID, zno(1 + k, 64), True, False)
                mm(ps(bank, W(128 + 64 * k, 64)), R(m), R("SG"), False, True)
        elif step == 2:
            for h in range(2):
                if t == 0:
                    act(R("LN", C(0, 2), h), ps(bank, W(128, 128)), ACT.Relu, bias=cf(B1 + h), scale=cf(MH + h))
                else:
                    ts(R("LN", C(0, 2), h), ps(bank, W(128, 128)), cf(MH + h), ALU.mult, 191.0, ALU.max)
        elif step == 3:
            for k in range(2):
                mm(ps(bank, W(256, 64)), R("LN", k), R("QL"), k == 0, k == 1)
        elif t == 0:
            lin(R("OUTB", C(0, 4), C(0, 16), t), ps(bank, W(256, 64)), None, -1.0)
        else:
            ts(R("OUTB", C(0, 4), C(0, 16), t), ps(bank, W(256, 64)), -1.0 - 4 * 191, ALU.add)

    VC = ((28, 28, 26, 30), (28, 28, 28, 34))
    tab = R("S", C(0, 8192))

    for t in range(2):
        def ot(q, a, b): return R("OT%d" % t, C(64 * q + a, 64 * q + b))
        for q in range(4):
            vc = VC[t][q]
            ts(R("GV", W(1024 * q, 16 * vc)), IND(tab, ot(q, 0, vc)), 0.0, ALU.max)
            act(R("GV", C(1024 * q + 16 * vc, 1024 * q + 1024)), IND(tab, ot(q, vc, 64)), ACT.Relu)
            if q > 0:
                scan(R("SC", W(256 * q - 256, 256)), R("D0"), ps(q - 1, C(0, 256)), 0.0, ALU.add, ALU.min)
            if q == 0:
                cutsome(t, 4)
            for l in range(8):
                mm(keys(q, l), R("GV", C(1024 * q + l, 1024 * q + 1024, 8)), R("SUMR"), False, l == 7 or (q, l) == (3, 3))
            cutsome(t, 2 if q < 3 else 3)
            if t == 0 and q < 3:
                ties(0, q + 1)
        if t == 0:
            lists_stage(1, 6)
        for a in range(2):
            scan(R("SC", W(768 + 128 * a, 128)), R("D0", C(0, 128)), ps(3 + 2 * a, W(128 * a, 128)), 0.0, ALU.add, ALU.min)
        if t == 1:
            cutev(0, CUTB[0])
            cutev(1, CUTB[1])
        else:
            constants_r(0)
            constants_late()
        mm(ps(2, C(0, 256)), R("BA", (0, 16)), R("MC", (0, 16)), True, False)
        for h in range(2):
            ts(R("YI", C(0, 4), h), R("SC", C(16 * h + 15, 1024, 32)), 511, ALU.bitwise_and)
        for x in range(2):
            ts(R("LF", C(0, 8), x), R("YI"), 256.0, ALU.is_ge, cf(MX + x), ALU.mult)
        mm(ps(4, C(0, 128)), R("LF"), R("CC"))
        for x in range(2):
            ts(R("LY", C(0, 8), x), R("YI"), 256.0, ALU.subtract, cf(MX + x), ALU.mult)
        mm(ps(0, C(0, 64)), R("LY"), R("CC", C(0, 64)))
        cutsome(t, 1)
        copy(R("FP"), ps(4, C(0, 128)))
        lin(zno(1, 64), ps(0, C(0, 64)), 1.0 / 16, 160 - 7.5 / 16)
        act(R("YB"), ps(0, C(0, 64)), ACT.Copy)
        for x in range(4):
            mm(ps(2, W(64 * x, 64)), R("BON"), R("FP", C(64, 128)), False, x == 3)
        mm(ps(3, C(0, 64)), R("BO"), R("FP", C(64, 128)), True, False)
        mm(ps(3, C(0, 64)), R("UN"), R("FP", C(0, 64)), False, True)
        mm(ps(0, C(64, 128)), ID, R("YB"), True, False)
        mm(ps(0, C(64, 128)), R("IS"), zno(1, 64), False, True)
        for a in range(2):
            mm(ps(4 + 2 * a, C(256, 384)), R("BA", (0, 16)), R("BB", (0, 16), C(0, 128)), True, False)
        cutsome(t, 2)
        ts(R("IW"), ot(0, 0, 256), -1.0, ALU.mult, TOP, ALU.add)
        scan(R("SC3"), R("RC"), ps(2, C(0, 256)), 0.0, ALU.min, ALU.max)
        act(zno(0, 64), ps(3, C(0, 64)), ACT.Copy)
        lin(zno(2, 64), ps(0, C(64, 128)), None, 2720.0)
        if t == 1:
            newparts(1, 0)
            cutev(2, CUTB[2])
        else:
            constants_r(1)
        cols = R("SC3", C(63, 256, 64))
        ts(R("COLB"), cols, 63.0, ALU.min, cf(CB), ALU.add)
        ts(R("OFQ"), cols, 64.0, ALU.min)
        tt(R("EQ"), IND(zno(0), R("OFQ")), R("SIG"), ALU.is_equal)
        for q in range(4):
            mm(ps(5, W(4 * q, 4)), R("PQ", W(128 * q, 128)), R("COLB"))
        for q in range(4):
            mm(ps(3, W(128 + 64 * q, 64)), R("PQ", W(128 * q, 128)), R("EQ"))
        copy(R("OFC"), ps(5, C(0, 16)))
        tt(R("EN"), IND(zno(1), R("OFQ")), R("EQ"), ALU.mult)
        act(R("E", C(128, 256)), IND(R("IW"), R("OFC", W(8, 8))), ACT.Copy)

        def parts(on):
            if on == 0:
                tt(R("EO"), IND(zno(2), R("OFQ")), R("EQ"), ALU.mult)
            for q in range(4):
                mm(ps(0, W(128 + 64 * (q % 2), 64)), bq(q, 2 * on + q // 2), R(("EO", "EN")[on]), on == 1 and q == 0,
                   on == 0 and q == 3)
            if on == 0:
                act(R("RR"), ps(0, C(128, 256)), ACT.Relu, bias=cf(RB))

        def lanes(a):
            tt(R("EI", W(128 * a, 128)), R("E", W(128 * a, 128)), ps(3, W(128 + 128 * a, 128)), ALU.mult)
            mm(ps(4 + 2 * a, C(256, 384)), R("BOW", W(32 - 32 * t, 128)), R("EI", W(128 * a, 128)), False, True)

        def change():
            for a in range(2):
                mm(ps(2, W(128 * a, 128)), R("DLH", W(128 * a, 128)), R("RR"))
            act(R("DL"), ps(2, C(0, 256)), ACT.Copy)

        if t == 1:
            newparts(1, 1)
        else:
            constants_r(2)
        parts(1)
        parts(0)
        copy(R("E", C(0, 128)), IND(R("IW"), R("OFC", W(0, 8))))
        lanes(0)
        change()
        lanes(1)
        if t == 1:
            cutev(3, CUTB[3])
            newparts(1, 2)
            newparts(1, 3)
        for a in range(2):
            scan(R("SC2", W(128 * a, 128)), R("D2", W(128 * a, 128)), ps(4 + 2 * a, C(256, 384)), 1000000.0, ALU.min, ALU.max)
        ends = R("SC2", C(15, 256, 16))

        def offs(o, i): ts(o, i, -1.0, ALU.mult, TOP, ALU.add)
        offs(R("OF", C(0, 16)), ends)
        for k in range(2 + t):
            mm(ps(3, W(16 * k, 16)), R("IWR", W(32 * k + 32, 128)), ends)
        if t == 0:
            for k in range(3):
                off = R("OF", W(16 * k, 16))
                copy(R("TMP", C(0, 128)), IND(R("S"), R("OF", W(16 * k, 8))))
                act(R("TMP", C(128, 256)), IND(R("S"), R("OF", W(16 * k + 8, 8))), ACT.Copy)
                if k == 0:
                    offs(R("OF", C(16, 48)), ps(3, C(0, 32)))
                if k == 2:
                    lin(R("CSW", C(96, 128)), R("SUMR"), 1.0 / 512)
                if k == 2:
                    newparts(0, 4)
                tt(IND(R("S"), off), R("TMP"), R("DL"), ALU.add)
                if k == 0:
                    newparts(0, 0)
                    newparts(0, 1)
                    for q in range(4):
                        ties(1, q)
                if k == 2:
                    act(spare(2048, 512), R("WB"), ACT.Identity, acc=R("WS", C(0, 1)))
                if k == 1:
                    for a, v in ((B1, -191.0), (HS4, -0.25), (HSM, -1.0)):
                        lin(cf(a, 2), cf(MH, 2), v)
                    newparts(0, 2)
                    newparts(0, 3)
        else:
            newparts(1, 4)
            send("anp", lambda s: R("OUTB", s), slot("NPR", 32))
            copy(IND(R("M"), R("OF", C(0, 16))), R("DL"))
            act(R("TMP"), IND(R("S"), R("OF", C(0, 16))), ACT.Copy)
            offs(R("OF", C(16, 64)), ps(3, C(0, 48)))
            sums = ((6, "IM", 0, 128), (0, "IP", 0, 256), (7, "IM", 128, 128))
            for bank, m, a, n in sums:
                mm(ps(bank, W(a, n)), ID, R("TMP", W(a, n)), True, False)
                mm(ps(bank, W(a, n)), R(m), R("DL", W(a, n)), False, False)
            fin = ps(5, (0, 2), C(0, 1))
            mm(fin, R("HW"), R("WS", C(0, 1)), True, False)
            for b in range(4):
                mm(fin, cf(HS4, 2), R("CACC", W(b, 1)), False, False)
            for k in (1, 2, 3):
                copy(R("MG", W(256 * k - 256, 128)), IND(R("M"), R("OF", W(16 * k, 8))))
                act(R("MG", W(256 * k - 128, 128)), IND(R("M"), R("OF", W(16 * k + 8, 8))), ACT.Copy)
                for bank, a in ((6, 0), (0, 0), (0, 1), (7, 1)):
                    mm(ps(bank, W(128 * a, 128)), R("IZ", W(96 - 32 * k, 128)), R("MG", W(256 * k - 256 + 128 * a, 128)),
                       False, k == 3 and (bank > 0 or a == 1))
            ts(R("RL"), ps(6, C(0, 128)), -1024.0, ALU.add, 0.0, ALU.max)
            act(spare(2560, 256), ps(0, C(0, 256)), ACT.Relu, bias=-1024.0, acc=R("FD", C(1, 2)))
            act(spare(2816, 128), ps(7, C(128, 256)), ACT.Relu, bias=-1024.0, acc=R("FD", C(2, 3)))
            fd, rl = R("FD", C(0, 1)), R("RL")
            emit("V", lambda: g.vector.tensor_reduce(fd[0], rl[0], AxisListType.X, ALU.add), [fd], [rl])
            mm(fin, cf(HSM, 2), R("FD", C(1, 2)), False, False)
            mm(fin, cf(MH, 2), fd, False, False)
            mm(fin, cf(MH, 2), R("FD", C(2, 3)), False, True)
            copy(R("CUTS", (0, 2), C(0, 1)), fin)
            send("acut", lambda s: R("CUTS", C(0, 1)), lambda s: R("CUTR", W(4 * s, 1)))
            dma("Y", T.newpart[2 * d:2 * d + 2, :], R("OUTB", d))
            dma("S", T.cut[2 * d:2 * d + 2, :], R("CUTS", (0, 2), C(0, 1)))
            for s in others:
                dma("Y", T.newpart[2 * s:2 * s + 2, :], slot("NPR", 32)(s))
            for s in others:
                dma("Y" if s == others[1] else "S", T.cut[2 * s:2 * s + 2, :], R("CUTR", (0, 2), W(4 * s, 1)))
    for s, v in total.items():
        if not any(seen[q].get(s, 0) >= v for q in seen):
            wait("G", s, v)
